import numpy as np
import ml_dtypes


def mxq(x, axis, fmt="e4m3"):
    dtype, down = {"e4m3": (ml_dtypes.float8_e4m3fn, 7), "e5m2": (ml_dtypes.float8_e5m2, 14)}[fmt]
    v = np.moveaxis(np.asarray(x, np.float32).astype(ml_dtypes.bfloat16).astype(np.float64), axis, -1)
    blocks = v.reshape(v.shape[:-1] + (-1, 32))
    amax = np.abs(blocks).max(-1, keepdims=True)
    byte = np.maximum(np.where(amax > 0, np.frexp(amax)[1] - 1 + 127, 0) - down, 1)
    scale = np.exp2(byte - 127.0)
    codes = (blocks / scale).astype(np.float32).astype(dtype).astype(np.float64)
    return np.moveaxis((codes * scale).reshape(v.shape), -1, axis)


WIDE = False


def mx_kscale(k):
    if not WIDE:
        return np.ones(k)
    levels = np.array([10, -10, 5, -5, 0])
    if k % 512:
        return np.exp2(np.random.permutation(np.resize(levels, k // 32))).repeat(32)
    a = np.empty((k // 512, 16))
    for p in range(k // 512):
        a[p, :8] = np.random.permutation(np.resize(levels, 8))
        for g in range(8):
            far = levels[np.abs(levels - a[p, g]) >= 10]
            a[p, g + 8] = far[np.random.randint(len(far))]
    return np.exp2(a.ravel()).repeat(32)


def f64(x):
    return np.asarray(x).astype(np.float64)


def striped(idx):
    return np.tile(idx.reshape(-1, 16).T, (8, 1)).astype(np.uint16)


def unstriped(offs):
    return offs[:16].T.reshape(-1).astype(np.int64)


E2M1 = np.array([0.0, 0.5, 1.0, 1.5, 2.0, 3.0, 4.0, 6.0, -0.0, -0.5, -1.0, -1.5, -2.0, -3.0, -4.0, -6.0])


def pack_weight(w, fmt):
    k, n = w.shape
    w = f64(np.asarray(w, np.float32).astype(ml_dtypes.bfloat16)).reshape(k // 32, 32, n)
    amax = np.abs(w).max(1)
    if fmt == "e4m3":
        byte = np.frexp(amax)[1] - 1 + 127 - 7
    else:
        mant, ex = np.frexp(amax / 6.0)
        byte = np.where(mant > 0.5, ex, ex - 1) + 127
    byte = np.clip(np.where(amax > 0, byte, 1), 1, 254)
    scaled = (w * np.exp2(127.0 - byte)[:, None, :]).reshape(k, n).astype(np.float32)
    by_word = np.ascontiguousarray(scaled.reshape(k // 512, 128, 4, n).transpose(0, 1, 3, 2))
    if fmt == "e4m3":
        words = by_word.astype(ml_dtypes.float8_e4m3fn).view(np.uint8)
    else:
        c = by_word.astype(ml_dtypes.float4_e2m1fn).view(np.uint8) & 0xF
        words = (c[..., 0::2] | (c[..., 1::2] << 4)).reshape(k // 512, 128, 2 * n)
    return np.ascontiguousarray(words), np.ascontiguousarray(byte.astype(np.uint8).reshape(k // 512, 16, n))


def unpack_weight(words, scales, fmt):
    g, _, n = scales.shape
    words = np.ascontiguousarray(words).reshape(g, 128, n, -1)
    if fmt == "e4m3":
        vals = words.view(ml_dtypes.float8_e4m3fn).astype(np.float64)
    else:
        nib = np.empty((g, 128, n, 4), np.uint8)
        nib[..., 0::2] = words & 0xF
        nib[..., 1::2] = words >> 4
        vals = E2M1[nib]
    vals = vals * np.repeat(np.exp2(scales.astype(np.float64) - 127.0), 8, axis=1)[..., None]
    return vals.transpose(0, 1, 3, 2).reshape(g * 512, n)


def gelu(v):
    return 0.5 * v * (1.0 + np.tanh(np.sqrt(2.0 / np.pi) * (v + 0.044715 * v**3)))


K, T, S, H, T2, S2, T3, P = 512, 4096, 1024, 512, 2048, 512, 2048, 1024

def setup_inputs():
    n = np.random.standard_normal
    s = mx_kscale(K)[:, None]
    tab_words, tab_scales = pack_weight(n((K, T)) * s, "e4m3")
    tab2_words, tab2_scales = pack_weight(n((H, T3)) / np.sqrt(H) / s, "e4m3")
    wf_words, wf_scales = pack_weight(0.7 * n((K, H)) / np.sqrt(K) / s, "e2m1")
    return {
        "tab_words": tab_words, "tab_scales": tab_scales,
        "offs": striped(np.random.permutation(T)[:S]),
        "tab2_words": tab2_words, "tab2_scales": tab2_scales,
        "offs2": striped(np.random.permutation(T3)[:S2]),
        "offs3": striped(np.random.permutation(T2)[:S]),
        "offs4": striped(np.random.permutation(T2)[:P]),
        "w": (n((K, H)) / np.sqrt(K) / s).astype(np.float32),
        "wf_words": wf_words, "wf_scales": wf_scales,
        "gain": (np.exp(0.3 * n(H)) * s[:, 0]).astype(np.float32),
        "page0": (n((H, T2)) * s).astype(np.float32),
        "wgs": np.exp(0.3 * n((128, S))).astype(np.float32),
        "reach": np.exp(0.5 * n((S2, P))).astype(np.float32),
    }

def reference(tab_words, tab_scales, offs, tab2_words, tab2_scales, offs2, offs3, offs4,
              w, wf_words, wf_scales, gain, page0, wgs, reach):
    v = unpack_weight(tab_words, tab_scales, "e4m3")[:, unstriped(offs)]
    v2 = unpack_weight(tab2_words, tab2_scales, "e4m3")[:, unstriped(offs2)]
    wf = unpack_weight(wf_words, wf_scales, "e2m1")
    wq = mxq(f64(w), 0, "e4m3")
    g = f64(gain)[:, None]
    t1 = np.tanh(wq.T @ v + wf.T @ v)
    d1 = mxq(g * t1, 0, "e4m3")
    t2 = np.tanh(wq.T @ v + wf.T @ v + wq.T @ d1)
    h = 0.5 * g * (t1 + t2)
    page = f64(page0).copy()
    page[:, unstriped(offs3)] = np.tile(f64(wgs), (H // 128, 1)) * h
    e = v2.T @ mxq(page, 0, "e4m3")
    return e[:, unstriped(offs4)] * f64(reach)

@@ -1,0 +1,298 @@
+from contextlib import ExitStack
+
+import concourse.mybir as mybir
+
+K, T, S, H, T2, S2, T3, PICK = 512, 4096, 1024, 512, 2048, 512, 2048, 1024
+FLOPS = 2 * (5 * K * H * S + H * S2 * T2)
+
+F32 = mybir.dt.float32
+BF16 = mybir.dt.bfloat16
+I32 = mybir.dt.int32
+U32 = mybir.dt.uint32
+U16 = mybir.dt.uint16
+U8 = mybir.dt.uint8
+FP8X4 = mybir.dt.float8_e4m3fn_x4
+FP4X4 = mybir.dt.float4_e2m1fn_x4
+MULT = mybir.AluOpType.mult
+ADD = mybir.AluOpType.add
+TANH = mybir.ActivationFunctionType.Tanh
+COPY = mybir.ActivationFunctionType.Copy
+
+P = 128
+PACK = 4
+N = 512
+PER_COL = 16
+
+
+def tile_list_lifeboat_heun_scores_kernel(
+    tc, tab_words, tab_scales, offs, tab2_words, tab2_scales, offs2, offs3, offs4,
+    w, wf_words, wf_scales, gain, page0, wgs, reach, out,
+):
+    nc = tc.nc
+    halves = S // N
+    chunks = T2 // N
+    boats = S2 // P
+
+    with ExitStack() as ctx:
+        keep = ctx.enter_context(tc.tile_pool(name="keep", bufs=1))
+        ring = ctx.enter_context(tc.tile_pool(name="ring", bufs=2))
+        psum = ctx.enter_context(tc.psum_pool(name="psum", bufs=1))
+
+        def held(name, shape, dtype):
+            return keep.tile(shape, dtype, name=name, align_bytes=64)
+
+        def bank(b):
+            return psum.tile([P, N], F32, name="bank%d" % b)
+
+        def load_scale_rows(queue, plane, rows):
+            for q in range(4):
+                queue.dma_start(
+                    out=plane[32 * q : 32 * q + 4, :].bitcast(I32),
+                    in_=rows[0, 4 * q : 4 * q + 4, :].bitcast(I32),
+                )
+
+        def words_of(table):
+            return table[0].rearrange("p n i -> p (n i)").bitcast(I32)
+
+        def columns(lists, first, count):
+            return lists[:, first // PER_COL : (first + count) // PER_COL]
+
+        list1 = held("list1", [P, S // PER_COL], U16)
+        list2 = held("list2", [P, S2 // PER_COL], U16)
+        list3 = held("list3", [P, S // PER_COL], U16)
+        list4 = held("list4", [P, PICK // PER_COL], U16)
+        tab_w = held("tab_w", [P, T], I32)
+        tab_s = held("tab_s", [P, T], U8)
+        tab2_w = held("tab2_w", [P, T3], I32)
+        tab2_s = held("tab2_s", [P, T3], U8)
+        w_raw = held("w_raw", [P, PACK, H], F32)
+        wf_raw = held("wf_raw", [P, 2 * H], U8)
+        wf_s_raw = held("wf_s_raw", [P, H], U8)
+        gain_sb = held("gain_sb", [P, PACK], F32)
+        pages = [held("page%d" % t, [P, T2], F32) for t in range(PACK)]
+        wgs_sb = {(e, h): held("wgs%d%d" % (e, h), [P, 2, N], F32) for e in range(2) for h in range(halves)}
+        reach_sb = [held("reach%d" % n, [P, PICK], F32) for n in range(boats)]
+
+        nc.vector.memset(tab_s[:].bitcast(I32), 0)
+        nc.vector.memset(wf_s_raw[:].bitcast(I32), 0)
+        nc.vector.memset(tab2_s[:].bitcast(I32), 0)
+
+        gain_rows = gain.rearrange("(p t) -> p t", t=PACK)
+        nc.sync.dma_start(out=w_raw[:], in_=w.rearrange("(p j) c -> p j c", j=PACK))
+        nc.sync.dma_start(out=gain_sb[:96], in_=gain_rows[:96])
+        load_scale_rows(nc.sync, tab_s, tab_scales)
+        nc.sync.dma_start(list1[:], offs)
+        nc.sync.dma_start(out=tab_w[:, : T // 2], in_=words_of(tab_words)[:, : T // 2])
+        nc.sync.dma_start(out=wf_raw[:].bitcast(I32), in_=wf_words[0].bitcast(I32))
+        load_scale_rows(nc.sync, wf_s_raw, wf_scales)
+        nc.sync.dma_start(out=gain_sb[96:], in_=gain_rows[96:])
+        nc.sync.dma_start(out=tab_w[:, T // 2 :], in_=words_of(tab_words)[:, T // 2 :])
+        load_scale_rows(nc.gpsimd, tab2_s, tab2_scales)
+        page_rows = page0.rearrange("(p t) c -> t p c", t=PACK)
+        wgs_rows = wgs.rearrange("(m u e) j -> e m u j", u=2, e=2)
+
+        def load_wgs(e, h):
+            for q in (0, 2, 1, 3):
+                nc.sync.dma_start(out=wgs_sb[e, h][32 * q : 32 * q + 32], in_=wgs_rows[e, :, :, h * N : (h + 1) * N])
+
+        nc.sync.dma_start(out=pages[0][:], in_=page_rows[0])
+        nc.sync.dma_start(list2[:], offs2)
+        nc.sync.dma_start(list3[:], offs3)
+        load_wgs(0, 0)
+        nc.sync.dma_start(out=pages[2][:], in_=page_rows[2])
+        nc.sync.dma_start(out=tab2_w[:], in_=words_of(tab2_words))
+        load_wgs(0, 1)
+        load_wgs(1, 0)
+        nc.sync.dma_start(out=pages[3][:], in_=page_rows[3])
+        load_wgs(1, 1)
+        nc.sync.dma_start(out=pages[1][:], in_=page_rows[1])
+        nc.sync.dma_start(list4[:], offs4)
+        for n in range(boats):
+            nc.sync.dma_start(out=reach_sb[n][:], in_=reach[n * P : (n + 1) * P, :])
+
+        w_bf = held("w_bf", [P, PACK * H], BF16)
+        wq = held("wq", [P, H], U32)
+        wq_s = held("wq_s", [P, H], U8)
+        nc.vector.tensor_copy(
+            out=w_bf[:].rearrange("p (t m j) -> p m t j", t=PACK, j=PACK),
+            in_=w_raw[:].rearrange("p j (m t) -> p m t j", t=PACK),
+        )
+        v_w = [held("v_w%d" % h, [P, N], U32) for h in range(halves)]
+        v_s = [held("v_s%d" % h, [P, N], U8) for h in range(halves)]
+        nc.vector.tensor_copy(out=v_s[0][:], in_=tab_s[:].indirect(columns(list1, 0, N)))
+        nc.vector.quantize_mx(out=wq[:].bitcast(FP8X4), scales=wq_s[:], in_=w_bf[:])
+        wf = held("wf", [P, 2 * H], U8)
+        wf_s = held("wf_s", [P, H], U8)
+        nc.vector.tensor_copy(
+            out=wf[:].bitcast(U16).rearrange("p (t m) -> p t m", t=PACK),
+            in_=wf_raw[:].bitcast(U16).rearrange("p (m t) -> p t m", t=PACK),
+        )
+        nc.vector.tensor_copy(
+            out=wf_s[:].rearrange("p (t m) -> p t m", t=PACK),
+            in_=wf_s_raw[:].rearrange("p (m t) -> p t m", t=PACK),
+        )
+        half_gain = held("half_gain", [P, PACK], F32)
+        nc.vector.tensor_scalar(half_gain[:], gain_sb[:], 0.5, None, MULT)
+        nc.vector.tensor_copy(out=v_s[1][:], in_=tab_s[:].indirect(columns(list1, N, N)))
+        for h in range(halves):
+            nc.vector.tensor_copy(out=v_w[h][:], in_=tab_w[:].bitcast(U32).indirect(columns(list1, h * N, N)))
+
+        def pass_w(acc, t, codes, scales, start, stop):
+            nc.tensor.matmul_mx(
+                out=acc, lhsT=wq[:, t * P : (t + 1) * P].bitcast(FP8X4), lhsT_scale=wq_s[:, t * P : (t + 1) * P],
+                rhs=codes.bitcast(FP8X4), rhs_scale=scales, start=start, stop=stop,
+            )
+
+        def state_passes(acc, t, h, first, width, stop):
+            pass_w(acc, t, v_w[h][:, first : first + width], v_s[h][:, first : first + width], True, False)
+            piece = N if width == N else P
+            for lo in range(0, width, piece):
+                cols = slice(first + lo, first + lo + piece)
+                nc.tensor.matmul_mx(
+                    out=acc[:, lo : lo + piece],
+                    lhsT=wf[:, 2 * t * P : 2 * (t + 1) * P].bitcast(FP4X4), lhsT_scale=wf_s[:, t * P : (t + 1) * P],
+                    rhs=v_w[h][:, cols].bitcast(FP8X4), rhs_scale=v_s[h][:, cols],
+                    start=False, stop=stop and lo + piece == width,
+                )
+
+        Q = N // 2
+        step1 = [held("step1_%d" % h, [P, PACK, N], F32) for h in range(halves)]
+        d1 = [held("d1_%d" % h, [P, N], U32) for h in range(halves)]
+        d1_s = [held("d1_s%d" % h, [P, N], U8) for h in range(halves)]
+        z2 = {}
+        slope = [held("slope%d" % i, [P, N], F32) for i in range(4)]
+        shared = held("shared", [P, 2 * N], F32)
+        t2 = {
+            (0, 0, 0): slope[3][:, Q:], (0, 0, Q): slope[0][:, :Q], (0, 2, 0): slope[0][:, Q:], (0, 2, Q): slope[3][:, :Q],
+            (1, 0, 0): slope[1][:], (0, 3, 0): slope[1][:], (1, 2, 0): slope[2][:], (0, 1, 0): slope[2][:],
+            (1, 3, 0): slope[0][:], (1, 1, 0): slope[0][:],
+        }
+        incs = [held("inc%d" % i, [P, N], F32) for i in range(3)]
+
+        def open_second(b, h, t, first, width):
+            z2[h, t, first] = bank(b)
+            state_passes(z2[h, t, first][:, :width], t, h, first, width, False)
+
+        def second_slope(h, t, first, width):
+            cols = slice(first, first + width)
+            pass_w(z2[h, t, first][:, :width], t, d1[h][:, cols], d1_s[h][:, cols], False, True)
+            nc.scalar.activation(t2[h, t, first], z2[h, t, first][:, :width], TANH)
+
+        order = [(0, 0, 0, Q), (0, 2, 0, Q), (0, 0, Q, Q), (0, 2, Q, Q), (1, 0, 0, N), (1, 2, 0, N), (0, 3, 0, N), (1, 3, 0, N), (0, 1, 0, N), (1, 1, 0, N)]
+
+        def inc_of(i):
+            return shared[:, (i // 3) * N : (i // 3) * N + Q] if i in (0, 3) else incs[i % 3][:, : order[i][3]]
+
+        def increment(i):
+            h, t, first, width = order[i]
+            nc.vector.scalar_tensor_tensor(inc_of(i), t2[h, t, first], half_gain[:, t : t + 1], step1[h][:, t, first : first + width], MULT, ADD)
+
+        def scatter(i):
+            h, t, first, width = order[i]
+            nc.vector.tensor_tensor(pages[t][:].indirect(columns(list3, h * N + first, width)), inc_of(i), wgs_sb[t % 2, h][:, t // 2, first : first + width], MULT)
+
+        page_bf = [held("page_bf%d" % c, [P, N, PACK], BF16) for c in range(chunks)]
+
+        def round_plane(t, c):
+            nc.scalar.copy(out=page_bf[c][:, :, t], in_=pages[t][:, c * N : (c + 1) * N])
+
+        def first_quarter(q):
+            for u in range(2):
+                z1 = bank(2 * q + u)
+                for e in range(2):
+                    state_passes(z1[:, e * Q : (e + 1) * Q], 2 * u + e, 0, q * Q, Q, True)
+                nc.scalar.activation(step1[0][:, 2 * u : 2 * u + 2, q * Q : (q + 1) * Q], z1[:].rearrange("p (e n) -> p e n", e=2), TANH)
+
+        def d1_quarter(q):
+            cols = slice(q * Q, (q + 1) * Q)
+            for t in range(PACK):
+                nc.vector.tensor_scalar(step1[0][:, t, cols], step1[0][:, t, cols], half_gain[:, t : t + 1], None, MULT)
+            woven = held("woven%d" % q, [P, Q, PACK], BF16)
+            nc.vector.tensor_scalar(woven[:], step1[0][:, :, cols].rearrange("p t n -> p n t"), 2.0, None, MULT)
+            nc.vector.quantize_mx(out=d1[0][:, cols].bitcast(FP8X4), scales=d1_s[0][:, cols], in_=woven[:].rearrange("p n t -> p (n t)"))
+
+        first_quarter(0)
+        first_quarter(1)
+        for q in range(2):
+            open_second(4 + 2 * q, 0, 0, q * Q, Q)
+            open_second(5 + 2 * q, 0, 2, q * Q, Q)
+        d1_quarter(0)
+        second_slope(0, 0, 0, Q)
+        second_slope(0, 2, 0, Q)
+        d1_quarter(1)
+        second_slope(0, 0, Q, Q)
+        second_slope(0, 2, Q, Q)
+        increment(0)
+        increment(1)
+        scatter(0)
+        for t in range(PACK):
+            z1 = bank((0, 1, 4, 5)[t])
+            state_passes(z1[:], t, 1, 0, N, True)
+            nc.scalar.activation(step1[1][:, t, :], z1[:], TANH)
+        v2_w = held("v2_w", [P, S2], U32)
+        v2_s = held("v2_s", [P, S2], U8)
+        nc.vector.tensor_copy(out=v2_s[:], in_=tab2_s[:].indirect(list2[:]))
+        nc.vector.tensor_copy(out=v2_w[:], in_=tab2_w[:].bitcast(U32).indirect(list2[:]))
+        for t in range(PACK):
+            nc.scalar.activation(step1[1][:, t, :], step1[1][:, t, :], COPY, scale=half_gain[:, t : t + 1])
+        woven1 = shared[:].bitcast(BF16)
+        nc.scalar.activation(woven1.rearrange("p (n t) -> p n t", t=PACK), step1[1][:].rearrange("p t n -> p n t"), COPY, scale=2.0)
+        increment(2)
+        scatter(1)
+        scatter(2)
+        nc.vector.quantize_mx(out=d1[1][:].bitcast(FP8X4), scales=d1_s[1][:], in_=woven1)
+        increment(3)
+        for b, h, t in [(2, 1, 0), (3, 1, 2), (0, 1, 3)]:
+            open_second(b, h, t, 0, N)
+            second_slope(h, t, 0, N)
+        scatter(3)
+        increment(4)
+        open_second(1, 0, 3, 0, N)
+        second_slope(0, 3, 0, N)
+        increment(5)
+        open_second(6, 0, 1, 0, N)
+        second_slope(0, 1, 0, N)
+        scatter(4)
+        increment(6)
+        for c in range(chunks):
+            round_plane(0, c)
+        scatter(5)
+        increment(7)
+        open_second(7, 1, 1, 0, N)
+        second_slope(1, 1, 0, N)
+        for c in range(chunks):
+            round_plane(2, c)
+        scatter(6)
+        increment(8)
+        scatter(7)
+        increment(9)
+        for c in range(chunks):
+            round_plane(3, c)
+        scatter(8)
+        scatter(9)
+
+        page_q = [held("page_q%d" % c, [P, N], U32) for c in range(chunks)]
+        page_s = [held("page_s%d" % c, [P, N], U8) for c in range(chunks)]
+        for c in (2, 3):
+            round_plane(1, c)
+        for c in (0, 1):
+            nc.vector.tensor_copy(out=page_bf[c][:, :, 1], in_=pages[1][:, c * N : (c + 1) * N])
+        for c in range(chunks):
+            nc.vector.quantize_mx(out=page_q[c][:].bitcast(FP8X4), scales=page_s[c][:], in_=page_bf[c][:].rearrange("p n t -> p (n t)"))
+
+        for n in range(boats):
+            scores = ring.tile([P, T2], F32, name="scores", bufs=3)
+            for c in range(chunks):
+                acc = bank((n * chunks + c) % (2 * PACK))
+                nc.tensor.matmul_mx(
+                    out=acc[:], lhsT=v2_w[:, n * P : (n + 1) * P].bitcast(FP8X4), lhsT_scale=v2_s[:, n * P : (n + 1) * P],
+                    rhs=page_q[c][:].bitcast(FP8X4), rhs_scale=page_s[c][:], start=True, stop=True,
+                )
+                if (n, c) == (0, chunks - 1):
+                    nc.vector.tensor_copy(out=scores[:, c * N : (c + 1) * N], in_=acc[:])
+                else:
+                    nc.scalar.copy(out=scores[:, c * N : (c + 1) * N], in_=acc[:])
+            for h in range(PICK // N):
+                picked = ring.tile([P, N], F32, name="picked", bufs=4)
+                nc.vector.tensor_tensor(picked[:], scores[:].indirect(columns(list4, h * N, N)), reach_sb[n][:, h * N : (h + 1) * N], MULT)
+                nc.sync.dma_start(out=out[n * P : (n + 1) * P, h * N : (h + 1) * N], in_=picked[:])

@@ -87,7 +87,7 @@ def tile_list_lifeboat_heun_scores_kernel(
         load_scale_rows(nc.sync, wf_s_raw, wf_scales)
         nc.sync.dma_start(out=gain_sb[96:], in_=gain_rows[96:])
         nc.sync.dma_start(out=tab_w[:, T // 2 :], in_=words_of(tab_words)[:, T // 2 :])
-        load_scale_rows(nc.gpsimd, tab2_s, tab2_scales)
+        load_scale_rows(nc.sync, tab2_s, tab2_scales)
         page_rows = page0.rearrange("(p t) c -> t p c", t=PACK)
         wgs_rows = wgs.rearrange("(m u e) j -> e m u j", u=2, e=2)
 
@@ -95,12 +95,12 @@ def tile_list_lifeboat_heun_scores_kernel(
             for q in (0, 2, 1, 3):
                 nc.sync.dma_start(out=wgs_sb[e, h][32 * q : 32 * q + 32], in_=wgs_rows[e, :, :, h * N : (h + 1) * N])
 
-        nc.sync.dma_start(out=pages[0][:], in_=page_rows[0])
         nc.sync.dma_start(list2[:], offs2)
+        nc.sync.dma_start(out=tab2_w[:], in_=words_of(tab2_words))
         nc.sync.dma_start(list3[:], offs3)
+        nc.sync.dma_start(out=pages[0][:], in_=page_rows[0])
         load_wgs(0, 0)
         nc.sync.dma_start(out=pages[2][:], in_=page_rows[2])
-        nc.sync.dma_start(out=tab2_w[:], in_=words_of(tab2_words))
         load_wgs(0, 1)
         load_wgs(1, 0)
         nc.sync.dma_start(out=pages[3][:], in_=page_rows[3])
@@ -110,17 +110,18 @@ def tile_list_lifeboat_heun_scores_kernel(
         for n in range(boats):
             nc.sync.dma_start(out=reach_sb[n][:], in_=reach[n * P : (n + 1) * P, :])
 
-        w_bf = held("w_bf", [P, PACK * H], BF16)
+        w_bf = [held("w_bf%d" % u, [P, 2 * H], BF16) for u in range(2)]
         wq = held("wq", [P, H], U32)
         wq_s = held("wq_s", [P, H], U8)
-        nc.vector.tensor_copy(
-            out=w_bf[:].rearrange("p (t m j) -> p m t j", t=PACK, j=PACK),
-            in_=w_raw[:].rearrange("p j (m t) -> p m t j", t=PACK),
-        )
+        w_in = w_raw[:].rearrange("p j (m t) -> p t m j", t=PACK)
+        nc.vector.tensor_copy(out=w_bf[0][:].rearrange("p (t m j) -> p m t j", t=2, j=PACK), in_=w_in[:, :2].rearrange("p t m j -> p m t j"))
+        nc.scalar.copy(out=w_bf[1][:].rearrange("p (t m j) -> p t m j", t=2, j=PACK), in_=w_in[:, 2:])
         v_w = [held("v_w%d" % h, [P, N], U32) for h in range(halves)]
         v_s = [held("v_s%d" % h, [P, N], U8) for h in range(halves)]
         nc.vector.tensor_copy(out=v_s[0][:], in_=tab_s[:].indirect(columns(list1, 0, N)))
-        nc.vector.quantize_mx(out=wq[:].bitcast(FP8X4), scales=wq_s[:], in_=w_bf[:])
+        for u in range(2):
+            cols = slice(u * H // 2, (u + 1) * H // 2)
+            nc.vector.quantize_mx(out=wq[:, cols].bitcast(FP8X4), scales=wq_s[:, cols], in_=w_bf[u][:])
         wf = held("wf", [P, 2 * H], U8)
         wf_s = held("wf_s", [P, H], U8)
         nc.vector.tensor_copy(
@@ -206,17 +207,20 @@ def tile_list_lifeboat_heun_scores_kernel(
         def d1_quarter(q):
             cols = slice(q * Q, (q + 1) * Q)
             for t in range(PACK):
-                nc.vector.tensor_scalar(step1[0][:, t, cols], step1[0][:, t, cols], half_gain[:, t : t + 1], None, MULT)
+                if q == 0:
+                    nc.scalar.activation(step1[0][:, t, cols], step1[0][:, t, cols], COPY, scale=half_gain[:, t : t + 1])
+                else:
+                    nc.vector.tensor_scalar(step1[0][:, t, cols], step1[0][:, t, cols], half_gain[:, t : t + 1], None, MULT)
             woven = held("woven%d" % q, [P, Q, PACK], BF16)
             nc.vector.tensor_scalar(woven[:], step1[0][:, :, cols].rearrange("p t n -> p n t"), 2.0, None, MULT)
             nc.vector.quantize_mx(out=d1[0][:, cols].bitcast(FP8X4), scales=d1_s[0][:, cols], in_=woven[:].rearrange("p n t -> p (n t)"))
 
         first_quarter(0)
+        d1_quarter(0)
         first_quarter(1)
         for q in range(2):
             open_second(4 + 2 * q, 0, 0, q * Q, Q)
             open_second(5 + 2 * q, 0, 2, q * Q, Q)
-        d1_quarter(0)
         second_slope(0, 0, 0, Q)
         second_slope(0, 2, 0, Q)
         d1_quarter(1)
@@ -273,26 +277,46 @@ def tile_list_lifeboat_heun_scores_kernel(
 
         page_q = [held("page_q%d" % c, [P, N], U32) for c in range(chunks)]
         page_s = [held("page_s%d" % c, [P, N], U8) for c in range(chunks)]
-        for c in (2, 3):
-            round_plane(1, c)
-        for c in (0, 1):
-            nc.vector.tensor_copy(out=page_bf[c][:, :, 1], in_=pages[1][:, c * N : (c + 1) * N])
-        for c in range(chunks):
-            nc.vector.quantize_mx(out=page_q[c][:].bitcast(FP8X4), scales=page_s[c][:], in_=page_bf[c][:].rearrange("p n t -> p (n t)"))
+        def last_plane(copy, c, first, width):
+            copy(out=page_bf[c][:, first : first + width, 1], in_=pages[1][:, c * N + first : c * N + first + width])
+
+        def quantise_page(c, first, width):
+            cols = slice(first, first + width)
+            nc.vector.quantize_mx(out=page_q[c][:, cols].bitcast(FP8X4), scales=page_s[c][:, cols], in_=page_bf[c][:, cols, :].rearrange("p n t -> p (n t)"))
+
+        last_plane(nc.scalar.copy, 3, 0, N)
+        last_plane(nc.scalar.copy, 2, Q, Q)
+        last_plane(nc.vector.tensor_copy, 0, 0, N)
+        last_plane(nc.vector.tensor_copy, 1, 0, N)
+        quantise_page(0, 0, N)
+        last_plane(nc.vector.tensor_copy, 2, 0, Q)
+        quantise_page(1, 0, N)
+        quantise_page(2, 0, Q)
+        quantise_page(3, 0, N)
+        quantise_page(2, Q, Q)
+
+        def score(b, scores, n, first, width, copy):
+            acc = bank(b)
+            c, lo = divmod(first, N)
+            nc.tensor.matmul_mx(
+                out=acc[:, :width], lhsT=v2_w[:, n * P : (n + 1) * P].bitcast(FP8X4), lhsT_scale=v2_s[:, n * P : (n + 1) * P],
+                rhs=page_q[c][:, lo : lo + width].bitcast(FP8X4), rhs_scale=page_s[c][:, lo : lo + width], start=True, stop=True,
+            )
+            copy(out=scores[:, first : first + width], in_=acc[:, :width])
 
         for n in range(boats):
             scores = ring.tile([P, T2], F32, name="scores", bufs=3)
-            for c in range(chunks):
-                acc = bank((n * chunks + c) % (2 * PACK))
-                nc.tensor.matmul_mx(
-                    out=acc[:], lhsT=v2_w[:, n * P : (n + 1) * P].bitcast(FP8X4), lhsT_scale=v2_s[:, n * P : (n + 1) * P],
-                    rhs=page_q[c][:].bitcast(FP8X4), rhs_scale=page_s[c][:], start=True, stop=True,
-                )
-                if (n, c) == (0, chunks - 1):
-                    nc.vector.tensor_copy(out=scores[:, c * N : (c + 1) * N], in_=acc[:])
-                else:
-                    nc.scalar.copy(out=scores[:, c * N : (c + 1) * N], in_=acc[:])
-            for h in range(PICK // N):
-                picked = ring.tile([P, N], F32, name="picked", bufs=4)
-                nc.vector.tensor_tensor(picked[:], scores[:].indirect(columns(list4, h * N, N)), reach_sb[n][:, h * N : (h + 1) * N], MULT)
-                nc.sync.dma_start(out=out[n * P : (n + 1) * P, h * N : (h + 1) * N], in_=picked[:])
+            if n == 0:
+                score(0, scores, n, 0, N, nc.scalar.copy)
+                score(1, scores, n, N, N, nc.scalar.copy)
+                score(4, scores, n, 2 * N, Q, nc.scalar.copy)
+                score(2, scores, n, 3 * N, N, nc.scalar.copy)
+                score(3, scores, n, 2 * N + Q, Q, nc.vector.tensor_copy)
+            else:
+                for b, c in ((0, 3), (2, 0), (3, 1), (1, 2)):
+                    score(b, scores, n, c * N, N, nc.scalar.copy)
+            pieces = [(0, PICK)] if n < boats - 1 else [(0, N), (N, Q), (N + Q, Q)]
+            for first, width in pieces:
+                picked = held("picked%d_%d" % (n, first), [P, width], F32)
+                nc.vector.tensor_tensor(picked[:], scores[:].indirect(columns(list4, first, width)), reach_sb[n][:, first : first + width], MULT)
+                nc.sync.dma_start(out=out[n * P : (n + 1) * P, first : first + width], in_=picked[:])

@@ -187,10 +187,11 @@ def tile_list_lifeboat_heun_scores_kernel(
         def increment(i):
             h, t, first, width = order[i]
             nc.vector.scalar_tensor_tensor(inc_of(i), t2[h, t, first], half_gain[:, t : t + 1], step1[h][:, t, first : first + width], MULT, ADD)
+            nc.gpsimd.tensor_tensor(inc_of(i), inc_of(i), wgs_sb[t % 2, h][:, t // 2, first : first + width], MULT)
 
         def scatter(i):
             h, t, first, width = order[i]
-            nc.vector.tensor_tensor(pages[t][:].indirect(columns(list3, h * N + first, width)), inc_of(i), wgs_sb[t % 2, h][:, t // 2, first : first + width], MULT)
+            nc.vector.tensor_copy(pages[t][:].indirect(columns(list3, h * N + first, width)), inc_of(i))
 
         page_bf = [held("page_bf%d" % c, [P, N, PACK], BF16) for c in range(chunks)]
 

@@ -21,6 +21,7 @@ COPY = mybir.ActivationFunctionType.Copy
 P = 128
 PACK = 4
 N = 512
+Q = N // 2
 PER_COL = 16
 
 
@@ -35,7 +36,6 @@ def tile_list_lifeboat_heun_scores_kernel(
 
     with ExitStack() as ctx:
         keep = ctx.enter_context(tc.tile_pool(name="keep", bufs=1))
-        ring = ctx.enter_context(tc.tile_pool(name="ring", bufs=2))
         psum = ctx.enter_context(tc.psum_pool(name="psum", bufs=1))
 
         def held(name, shape, dtype):
@@ -44,7 +44,7 @@ def tile_list_lifeboat_heun_scores_kernel(
         def bank(b):
             return psum.tile([P, N], F32, name="bank%d" % b)
 
-        def load_scale_rows(queue, plane, rows):
+        def load_scale_rows(plane, rows, queue=nc.sync):
             for q in range(4):
                 queue.dma_start(
                     out=plane[32 * q : 32 * q + 4, :].bitcast(I32),
@@ -70,42 +70,39 @@ def tile_list_lifeboat_heun_scores_kernel(
         wf_s_raw = held("wf_s_raw", [P, H], U8)
         gain_sb = held("gain_sb", [P, PACK], F32)
         pages = [held("page%d" % t, [P, T2], F32) for t in range(PACK)]
-        wgs_sb = {(e, h): held("wgs%d%d" % (e, h), [P, 2, N], F32) for e in range(2) for h in range(halves)}
+        wgs_sb = {(u, h): held("wgs%d%d" % (u, h), [P, 2, N], F32) for u in range(2) for h in range(halves)}
         reach_sb = [held("reach%d" % n, [P, PICK], F32) for n in range(boats)]
 
         nc.vector.memset(tab_s[:].bitcast(I32), 0)
         nc.vector.memset(wf_s_raw[:].bitcast(I32), 0)
         nc.vector.memset(tab2_s[:].bitcast(I32), 0)
 
-        gain_rows = gain.rearrange("(p t) -> p t", t=PACK)
-        nc.sync.dma_start(out=w_raw[:], in_=w.rearrange("(p j) c -> p j c", j=PACK))
-        nc.sync.dma_start(out=gain_sb[:96], in_=gain_rows[:96])
-        load_scale_rows(nc.sync, tab_s, tab_scales)
-        nc.sync.dma_start(list1[:], offs)
-        nc.sync.dma_start(out=tab_w[:, : T // 2], in_=words_of(tab_words)[:, : T // 2])
-        nc.sync.dma_start(out=wf_raw[:].bitcast(I32), in_=wf_words[0].bitcast(I32))
-        load_scale_rows(nc.sync, wf_s_raw, wf_scales)
-        nc.sync.dma_start(out=gain_sb[96:], in_=gain_rows[96:])
-        nc.sync.dma_start(out=tab_w[:, T // 2 :], in_=words_of(tab_words)[:, T // 2 :])
-        load_scale_rows(nc.sync, tab2_s, tab2_scales)
         page_rows = page0.rearrange("(p t) c -> t p c", t=PACK)
-        wgs_rows = wgs.rearrange("(m u e) j -> e m u j", u=2, e=2)
+        wgs_rows = wgs.rearrange("(m u e) j -> u m e j", u=2, e=2)
 
-        def load_wgs(e, h):
+        def load_wgs(u, h):
             for q in (0, 2, 1, 3):
-                nc.sync.dma_start(out=wgs_sb[e, h][32 * q : 32 * q + 32], in_=wgs_rows[e, :, :, h * N : (h + 1) * N])
+                nc.sync.dma_start(out=wgs_sb[u, h][32 * q : 32 * q + 32], in_=wgs_rows[u, :, :, h * N : (h + 1) * N])
 
+        nc.sync.dma_start(out=w_raw[:], in_=w.rearrange("(p j) c -> p j c", j=PACK))
+        nc.sync.dma_start(list1[:], offs)
+        load_scale_rows(tab_s, tab_scales)
+        nc.sync.dma_start(out=wf_raw[:].bitcast(I32), in_=wf_words[0].bitcast(I32))
+        nc.sync.dma_start(out=tab_w[:], in_=words_of(tab_words))
+        load_scale_rows(wf_s_raw, wf_scales)
+        nc.sync.dma_start(out=gain_sb[:], in_=gain.rearrange("(p t) -> p t", t=PACK))
         nc.sync.dma_start(list2[:], offs2)
+        load_scale_rows(tab2_s, tab2_scales)
+        load_wgs(0, 0)
         nc.sync.dma_start(out=tab2_w[:], in_=words_of(tab2_words))
         nc.sync.dma_start(list3[:], offs3)
         nc.sync.dma_start(out=pages[0][:], in_=page_rows[0])
-        load_wgs(0, 0)
+        nc.sync.dma_start(out=pages[1][:], in_=page_rows[1])
+        load_wgs(1, 0)
         nc.sync.dma_start(out=pages[2][:], in_=page_rows[2])
         load_wgs(0, 1)
-        load_wgs(1, 0)
-        nc.sync.dma_start(out=pages[3][:], in_=page_rows[3])
         load_wgs(1, 1)
-        nc.sync.dma_start(out=pages[1][:], in_=page_rows[1])
+        nc.sync.dma_start(out=pages[3][:], in_=page_rows[3])
         nc.sync.dma_start(list4[:], offs4)
         for n in range(boats):
             nc.sync.dma_start(out=reach_sb[n][:], in_=reach[n * P : (n + 1) * P, :])
@@ -128,15 +125,19 @@ def tile_list_lifeboat_heun_scores_kernel(
             out=wf[:].bitcast(U16).rearrange("p (t m) -> p t m", t=PACK),
             in_=wf_raw[:].bitcast(U16).rearrange("p (m t) -> p t m", t=PACK),
         )
+        nc.vector.tensor_copy(out=v_s[1][:], in_=tab_s[:].indirect(columns(list1, N, N)))
+        nc.vector.tensor_copy(out=v_w[0][:], in_=tab_w[:].bitcast(U32).indirect(columns(list1, 0, N)))
         nc.vector.tensor_copy(
             out=wf_s[:].rearrange("p (t m) -> p t m", t=PACK),
             in_=wf_s_raw[:].rearrange("p (m t) -> p t m", t=PACK),
         )
-        half_gain = held("half_gain", [P, PACK], F32)
-        nc.vector.tensor_scalar(half_gain[:], gain_sb[:], 0.5, None, MULT)
-        nc.vector.tensor_copy(out=v_s[1][:], in_=tab_s[:].indirect(columns(list1, N, N)))
-        for h in range(halves):
-            nc.vector.tensor_copy(out=v_w[h][:], in_=tab_w[:].bitcast(U32).indirect(columns(list1, h * N, N)))
+        half_gain = {}
+        for name in ("both", "late_terms"):
+            half_gain[name] = held(name, [P, PACK], F32)
+            nc.vector.tensor_scalar(half_gain[name][:], gain_sb[:], 0.5, None, MULT)
+        nc.vector.tensor_copy(out=v_w[1][:], in_=tab_w[:].bitcast(U32).indirect(columns(list1, N, N)))
+        v2_s = held("v2_s", [P, S2], U8)
+        nc.vector.tensor_copy(out=v2_s[:], in_=tab2_s[:].indirect(list2[:]))
 
         def pass_w(acc, t, codes, scales, start, stop):
             nc.tensor.matmul_mx(
@@ -156,145 +157,143 @@ def tile_list_lifeboat_heun_scores_kernel(
                     start=False, stop=stop and lo + piece == width,
                 )
 
-        Q = N // 2
-        step1 = [held("step1_%d" % h, [P, PACK, N], F32) for h in range(halves)]
-        d1 = [held("d1_%d" % h, [P, N], U32) for h in range(halves)]
+        t1 = [held("t1_%d" % h, [P, PACK, N], F32) for h in range(halves)]
+        d1 = [held("d1_0", [P, N], U32)]
         d1_s = [held("d1_s%d" % h, [P, N], U8) for h in range(halves)]
         z2 = {}
-        slope = [held("slope%d" % i, [P, N], F32) for i in range(4)]
-        shared = held("shared", [P, 2 * N], F32)
-        t2 = {
-            (0, 0, 0): slope[3][:, Q:], (0, 0, Q): slope[0][:, :Q], (0, 2, 0): slope[0][:, Q:], (0, 2, Q): slope[3][:, :Q],
-            (1, 0, 0): slope[1][:], (0, 3, 0): slope[1][:], (1, 2, 0): slope[2][:], (0, 1, 0): slope[2][:],
-            (1, 3, 0): slope[0][:], (1, 1, 0): slope[0][:],
-        }
-        incs = [held("inc%d" % i, [P, N], F32) for i in range(3)]
+        term = {}
 
-        def open_second(b, h, t, first, width):
-            z2[h, t, first] = bank(b)
-            state_passes(z2[h, t, first][:, :width], t, h, first, width, False)
+        def weights_of(t, h):
+            return wgs_sb[t // 2, h][:, t % 2, :]
 
-        def second_slope(h, t, first, width):
+        def scale_weights_gpsimd(t, h, name):
+            nc.gpsimd.tensor_scalar(weights_of(t, h), weights_of(t, h), half_gain[name][:, t : t + 1], 0.0, MULT, ADD)
+
+        def scale_weights_scalar(t, h, name):
+            nc.scalar.activation(weights_of(t, h), weights_of(t, h), COPY, scale=half_gain[name][:, t : t + 1])
+
+        def open_second(b, t, h, first, width):
+            z2[t, h, first] = bank(b)
+            state_passes(z2[t, h, first][:, :width], t, h, first, width, False)
+
+        def second_slope(t, h, first, width):
             cols = slice(first, first + width)
-            pass_w(z2[h, t, first][:, :width], t, d1[h][:, cols], d1_s[h][:, cols], False, True)
-            nc.scalar.activation(t2[h, t, first], z2[h, t, first][:, :width], TANH)
+            pass_w(z2[t, h, first][:, :width], t, d1[h][:, cols], d1_s[h][:, cols], False, True)
+            if (t, h, first) not in term:
+                term[t, h, first] = held("term%d_%d_%d" % (t, h, first), [P, width], F32)[:]
+            nc.scalar.activation(term[t, h, first], z2[t, h, first][:, :width], TANH)
 
-        order = [(0, 0, 0, Q), (0, 2, 0, Q), (0, 0, Q, Q), (0, 2, Q, Q), (1, 0, 0, N), (1, 2, 0, N), (0, 3, 0, N), (1, 3, 0, N), (0, 1, 0, N), (1, 1, 0, N)]
+        def put(t, h, first, width):
+            cols = slice(first, first + width)
+            values = term[t, h, first]
+            both = held("both", [P, width], F32)
+            nc.gpsimd.tensor_tensor(both[:], values, t1[h][:, t, cols], ADD)
+            nc.gpsimd.tensor_tensor(values, both[:], weights_of(t, h)[:, cols], MULT)
+            nc.vector.tensor_copy(pages[t][:].indirect(columns(list3, h * N + first, width)), values)
 
-        def inc_of(i):
-            return shared[:, (i // 3) * N : (i // 3) * N + Q] if i in (0, 3) else incs[i % 3][:, : order[i][3]]
+        def quantise_d1(h, first, width, woven):
+            cols = slice(first, first + width)
+            nc.vector.quantize_mx(out=d1[h][:, cols].bitcast(FP8X4), scales=d1_s[h][:, cols], in_=woven[:].rearrange("p n t -> p (n t)"))
 
-        def increment(i):
-            h, t, first, width = order[i]
-            nc.vector.scalar_tensor_tensor(inc_of(i), t2[h, t, first], half_gain[:, t : t + 1], step1[h][:, t, first : first + width], MULT, ADD)
-            nc.gpsimd.tensor_tensor(inc_of(i), inc_of(i), wgs_sb[t % 2, h][:, t // 2, first : first + width], MULT)
-
-        def scatter(i):
-            h, t, first, width = order[i]
-            nc.vector.tensor_copy(pages[t][:].indirect(columns(list3, h * N + first, width)), inc_of(i))
+        warm = bank(7)
+        for i in range(5):
+            pass_w(warm[:], 0, wq[:], wq_s[:], True, True)
+        for t in range(2):
+            scale_weights_gpsimd(t, 0, "both")
+        woven0 = held("woven0", [P, Q, PACK], BF16)
+        for t in range(PACK):
+            z1 = bank(t)
+            state_passes(z1[:, :Q], t, 0, 0, Q, True)
+            nc.scalar.activation(t1[0][:, t, :Q], z1[:, :Q], TANH)
+            nc.vector.tensor_scalar(woven0[:, :, t], t1[0][:, t, :Q], gain_sb[:, t : t + 1], None, MULT)
+        quantise_d1(0, 0, Q, woven0)
+        for u in range(2):
+            z1 = bank(6 + u)
+            for e in range(2):
+                state_passes(z1[:, e * Q : (e + 1) * Q], 2 * u + e, 0, Q, Q, True)
+            nc.scalar.activation(t1[0][:, 2 * u : 2 * u + 2, Q:], z1[:].rearrange("p (e n) -> p e n", e=2), TANH)
+        for t in range(2):
+            open_second(4 + t, t, 0, 0, Q)
+        for t in range(2):
+            second_slope(t, 0, 0, Q)
+        woven1 = held("woven1", [P, Q, PACK], BF16)
+        nc.vector.tensor_tensor(woven1[:], t1[0][:, :, Q:].rearrange("p t n -> p n t"), gain_sb[:].unsqueeze(1).to_broadcast([P, Q, PACK]), MULT)
+        quantise_d1(0, Q, Q, woven1)
+        for t in range(2):
+            open_second(6 + t, t, 0, Q, Q)
+        for t in range(2):
+            second_slope(t, 0, Q, Q)
+        for t in range(PACK):
+            z1 = bank(t)
+            state_passes(z1[:], t, 1, 0, N, True)
+            nc.scalar.activation(t1[1][:, t, :], z1[:], TANH)
+        for t in range(2):
+            for first in (0, Q):
+                put(t, 0, first, Q)
+        flat = held("flat", [P, PACK, N], BF16)
+        for t in range(PACK):
+            nc.scalar.activation(flat[:, t, :], t1[1][:, t, :], COPY, scale=gain_sb[:, t : t + 1])
+        open_second(4, 2, 0, 0, N)
+        second_slope(2, 0, 0, N)
+        woven2 = held("woven2", [P, N, PACK], BF16)
+        nc.scalar.copy(out=woven2[:].rearrange("p (c i) t -> p c t i", i=4), in_=flat[:].rearrange("p t (c i) -> p c t i", i=4))
+        d1.append(held("term1_0_%d" % Q, [P, N], U32))
+        quantise_d1(1, 0, N, woven2)
+        v2_w = held("woven2", [P, S2], U32)
+        nc.vector.tensor_copy(out=v2_w[:], in_=tab2_w[:].bitcast(U32).indirect(list2[:]))
+        scale_weights_scalar(2, 0, "late_terms")
+        put(2, 0, 0, N)
+        for t, h in [(0, 1), (1, 1), (3, 0), (2, 1), (3, 1)]:
+            scale_weights_scalar(t, h, "late_terms")
+        late_terms = held("late_terms", [P, 5, N], F32)
+        for i, (t, h) in enumerate([(0, 1), (1, 1), (2, 1), (3, 0), (3, 1)]):
+            term[t, h, 0] = late_terms[:, i, :]
+        term[0, 1, 0], term[0, 1, Q] = late_terms[:, 0, :Q], late_terms[:, 0, Q:]
+        for b, first in [(5, 0), (6, Q)]:
+            open_second(b, 0, 1, first, Q)
+            second_slope(0, 1, first, Q)
+            put(0, 1, first, Q)
+        for b, t, h in [(0, 1, 1), (1, 2, 1), (2, 3, 0), (3, 3, 1)]:
+            open_second(b, t, h, 0, N)
+            second_slope(t, h, 0, N)
+            put(t, h, 0, N)
 
         page_bf = [held("page_bf%d" % c, [P, N, PACK], BF16) for c in range(chunks)]
+        rounded = held("both", [P, 2, T2], BF16)
 
-        def round_plane(t, c):
-            nc.scalar.copy(out=page_bf[c][:, :, t], in_=pages[t][:, c * N : (c + 1) * N])
+        def pair_write(copy, first, width):
+            c, lo = divmod(first, N)
+            copy(out=page_bf[c][:, lo : lo + width, 2:], in_=rounded[:, :, first : first + width].rearrange("p e n -> p n e"))
 
-        def first_quarter(q):
-            for u in range(2):
-                z1 = bank(2 * q + u)
-                for e in range(2):
-                    state_passes(z1[:, e * Q : (e + 1) * Q], 2 * u + e, 0, q * Q, Q, True)
-                nc.scalar.activation(step1[0][:, 2 * u : 2 * u + 2, q * Q : (q + 1) * Q], z1[:].rearrange("p (e n) -> p e n", e=2), TANH)
-
-        def d1_quarter(q):
-            cols = slice(q * Q, (q + 1) * Q)
-            for t in range(PACK):
-                if q == 0:
-                    nc.scalar.activation(step1[0][:, t, cols], step1[0][:, t, cols], COPY, scale=half_gain[:, t : t + 1])
-                else:
-                    nc.vector.tensor_scalar(step1[0][:, t, cols], step1[0][:, t, cols], half_gain[:, t : t + 1], None, MULT)
-            woven = held("woven%d" % q, [P, Q, PACK], BF16)
-            nc.vector.tensor_scalar(woven[:], step1[0][:, :, cols].rearrange("p t n -> p n t"), 2.0, None, MULT)
-            nc.vector.quantize_mx(out=d1[0][:, cols].bitcast(FP8X4), scales=d1_s[0][:, cols], in_=woven[:].rearrange("p n t -> p (n t)"))
-
-        first_quarter(0)
-        d1_quarter(0)
-        first_quarter(1)
-        for q in range(2):
-            open_second(4 + 2 * q, 0, 0, q * Q, Q)
-            open_second(5 + 2 * q, 0, 2, q * Q, Q)
-        second_slope(0, 0, 0, Q)
-        second_slope(0, 2, 0, Q)
-        d1_quarter(1)
-        second_slope(0, 0, Q, Q)
-        second_slope(0, 2, Q, Q)
-        increment(0)
-        increment(1)
-        scatter(0)
-        for t in range(PACK):
-            z1 = bank((0, 1, 4, 5)[t])
-            state_passes(z1[:], t, 1, 0, N, True)
-            nc.scalar.activation(step1[1][:, t, :], z1[:], TANH)
-        v2_w = held("v2_w", [P, S2], U32)
-        v2_s = held("v2_s", [P, S2], U8)
-        nc.vector.tensor_copy(out=v2_s[:], in_=tab2_s[:].indirect(list2[:]))
-        nc.vector.tensor_copy(out=v2_w[:], in_=tab2_w[:].bitcast(U32).indirect(list2[:]))
-        for t in range(PACK):
-            nc.scalar.activation(step1[1][:, t, :], step1[1][:, t, :], COPY, scale=half_gain[:, t : t + 1])
-        woven1 = shared[:].bitcast(BF16)
-        nc.scalar.activation(woven1.rearrange("p (n t) -> p n t", t=PACK), step1[1][:].rearrange("p t n -> p n t"), COPY, scale=2.0)
-        increment(2)
-        scatter(1)
-        scatter(2)
-        nc.vector.quantize_mx(out=d1[1][:].bitcast(FP8X4), scales=d1_s[1][:], in_=woven1)
-        increment(3)
-        for b, h, t in [(2, 1, 0), (3, 1, 2), (0, 1, 3)]:
-            open_second(b, h, t, 0, N)
-            second_slope(h, t, 0, N)
-        scatter(3)
-        increment(4)
-        open_second(1, 0, 3, 0, N)
-        second_slope(0, 3, 0, N)
-        increment(5)
-        open_second(6, 0, 1, 0, N)
-        second_slope(0, 1, 0, N)
-        scatter(4)
-        increment(6)
-        for c in range(chunks):
-            round_plane(0, c)
-        scatter(5)
-        increment(7)
-        open_second(7, 1, 1, 0, N)
-        second_slope(1, 1, 0, N)
-        for c in range(chunks):
-            round_plane(2, c)
-        scatter(6)
-        increment(8)
-        scatter(7)
-        increment(9)
-        for c in range(chunks):
-            round_plane(3, c)
-        scatter(8)
-        scatter(9)
+        for t in range(2):
+            for c in range(chunks):
+                nc.scalar.copy(out=page_bf[c][:, :, t], in_=pages[t][:, c * N : (c + 1) * N])
+        nc.gpsimd.tensor_scalar(rounded[:, 0, :], pages[2][:], 1.0, 0.0, MULT, ADD)
 
         page_q = [held("page_q%d" % c, [P, N], U32) for c in range(chunks)]
         page_s = [held("page_s%d" % c, [P, N], U8) for c in range(chunks)]
-        def last_plane(copy, c, first, width):
-            copy(out=page_bf[c][:, first : first + width, 1], in_=pages[1][:, c * N + first : c * N + first + width])
 
-        def quantise_page(c, first, width):
-            cols = slice(first, first + width)
+        def round_last(copy, first, width):
+            copy(out=rounded[:, 1, first : first + width], in_=pages[3][:, first : first + width])
+
+        def quantise_page(first, width):
+            c, lo = divmod(first, N)
+            cols = slice(lo, lo + width)
             nc.vector.quantize_mx(out=page_q[c][:, cols].bitcast(FP8X4), scales=page_s[c][:, cols], in_=page_bf[c][:, cols, :].rearrange("p n t -> p (n t)"))
 
-        last_plane(nc.scalar.copy, 3, 0, N)
-        last_plane(nc.scalar.copy, 2, Q, Q)
-        last_plane(nc.vector.tensor_copy, 0, 0, N)
-        last_plane(nc.vector.tensor_copy, 1, 0, N)
-        quantise_page(0, 0, N)
-        last_plane(nc.vector.tensor_copy, 2, 0, Q)
-        quantise_page(1, 0, N)
-        quantise_page(2, 0, Q)
-        quantise_page(3, 0, N)
-        quantise_page(2, Q, Q)
+        round_last(nc.scalar.copy, 2 * N + Q, N + Q)
+        pair_write(nc.scalar.copy, 3 * N, N)
+        pair_write(nc.scalar.copy, 2 * N + Q, Q)
+        round_last(nc.vector.tensor_copy, 0, N)
+        round_last(nc.vector.tensor_copy, N, N + Q)
+        pair_write(nc.vector.tensor_copy, 0, N)
+        pair_write(nc.vector.tensor_copy, N, N)
+        quantise_page(0, N)
+        pair_write(nc.vector.tensor_copy, 2 * N, Q)
+        quantise_page(N, N)
+        quantise_page(2 * N, Q)
+        quantise_page(3 * N, N)
+        quantise_page(2 * N + Q, Q)
 
         def score(b, scores, n, first, width, copy):
             acc = bank(b)
@@ -306,7 +305,7 @@ def tile_list_lifeboat_heun_scores_kernel(
             copy(out=scores[:, first : first + width], in_=acc[:, :width])
 
         for n in range(boats):
-            scores = ring.tile([P, T2], F32, name="scores", bufs=3)
+            scores = held(("scores0", "scores1", "w_raw")[n % 3], [P, T2], F32)
             if n == 0:
                 score(0, scores, n, 0, N, nc.scalar.copy)
                 score(1, scores, n, N, N, nc.scalar.copy)
@@ -318,6 +317,6 @@ def tile_list_lifeboat_heun_scores_kernel(
                     score(b, scores, n, c * N, N, nc.scalar.copy)
             pieces = [(0, PICK)] if n < boats - 1 else [(0, N), (N, Q), (N + Q, Q)]
             for first, width in pieces:
-                picked = held("picked%d_%d" % (n, first), [P, width], F32)
+                picked = held(("t1_0", "t1_1", "flat")[n] if n < boats - 1 else "picked%d" % first, [P, width], F32)
                 nc.vector.tensor_tensor(picked[:], scores[:].indirect(columns(list4, first, width)), reach_sb[n][:, first : first + width], MULT)
                 nc.sync.dma_start(out=out[n * P : (n + 1) * P, first : first + width], in_=picked[:])

@@ -91,18 +91,18 @@ def tile_list_lifeboat_heun_scores_kernel(
         nc.sync.dma_start(out=tab_w[:], in_=words_of(tab_words))
         load_scale_rows(wf_s_raw, wf_scales)
         nc.sync.dma_start(out=gain_sb[:], in_=gain.rearrange("(p t) -> p t", t=PACK))
+        load_wgs(0, 0)
         nc.sync.dma_start(list2[:], offs2)
         load_scale_rows(tab2_s, tab2_scales)
-        load_wgs(0, 0)
-        nc.sync.dma_start(out=tab2_w[:], in_=words_of(tab2_words))
         nc.sync.dma_start(list3[:], offs3)
         nc.sync.dma_start(out=pages[0][:], in_=page_rows[0])
         nc.sync.dma_start(out=pages[1][:], in_=page_rows[1])
         load_wgs(1, 0)
         nc.sync.dma_start(out=pages[2][:], in_=page_rows[2])
+        nc.sync.dma_start(out=tab2_w[:], in_=words_of(tab2_words))
         load_wgs(0, 1)
-        load_wgs(1, 1)
         nc.sync.dma_start(out=pages[3][:], in_=page_rows[3])
+        load_wgs(1, 1)
         nc.sync.dma_start(list4[:], offs4)
         for n in range(boats):
             nc.sync.dma_start(out=reach_sb[n][:], in_=reach[n * P : (n + 1) * P, :])
@@ -132,7 +132,7 @@ def tile_list_lifeboat_heun_scores_kernel(
             in_=wf_s_raw[:].rearrange("p (m t) -> p t m", t=PACK),
         )
         half_gain = {}
-        for name in ("both", "late_terms"):
+        for name in ("both", "late_terms", "page_bf"):
             half_gain[name] = held(name, [P, PACK], F32)
             nc.vector.tensor_scalar(half_gain[name][:], gain_sb[:], 0.5, None, MULT)
         nc.vector.tensor_copy(out=v_w[1][:], in_=tab_w[:].bitcast(U32).indirect(columns(list1, N, N)))
@@ -243,7 +243,7 @@ def tile_list_lifeboat_heun_scores_kernel(
         nc.vector.tensor_copy(out=v2_w[:], in_=tab2_w[:].bitcast(U32).indirect(list2[:]))
         scale_weights_scalar(2, 0, "late_terms")
         put(2, 0, 0, N)
-        for t, h in [(0, 1), (1, 1), (3, 0), (2, 1), (3, 1)]:
+        for t, h in [(0, 1), (1, 1), (3, 0)]:
             scale_weights_scalar(t, h, "late_terms")
         late_terms = held("late_terms", [P, 5, N], F32)
         for i, (t, h) in enumerate([(0, 1), (1, 1), (2, 1), (3, 0), (3, 1)]):
@@ -253,21 +253,22 @@ def tile_list_lifeboat_heun_scores_kernel(
             open_second(b, 0, 1, first, Q)
             second_slope(0, 1, first, Q)
             put(0, 1, first, Q)
-        for b, t, h in [(0, 1, 1), (1, 2, 1), (2, 3, 0), (3, 3, 1)]:
+        for b, t, h in [(0, 1, 1), (2, 3, 0), (1, 2, 1), (3, 3, 1)]:
             open_second(b, t, h, 0, N)
+            if (t // 2, h) == (1, 1):
+                scale_weights_scalar(t, h, "page_bf")
             second_slope(t, h, 0, N)
             put(t, h, 0, N)
 
-        page_bf = [held("page_bf%d" % c, [P, N, PACK], BF16) for c in range(chunks)]
+        page_bf = held("page_bf", [P, T2, PACK], BF16)
         rounded = held("both", [P, 2, T2], BF16)
 
         def pair_write(copy, first, width):
-            c, lo = divmod(first, N)
-            copy(out=page_bf[c][:, lo : lo + width, 2:], in_=rounded[:, :, first : first + width].rearrange("p e n -> p n e"))
+            copy(out=page_bf[:, first : first + width, 2:], in_=rounded[:, :, first : first + width].rearrange("p e n -> p n e"))
 
         for t in range(2):
             for c in range(chunks):
-                nc.scalar.copy(out=page_bf[c][:, :, t], in_=pages[t][:, c * N : (c + 1) * N])
+                nc.scalar.copy(out=page_bf[:, c * N : (c + 1) * N, t], in_=pages[t][:, c * N : (c + 1) * N])
         nc.gpsimd.tensor_scalar(rounded[:, 0, :], pages[2][:], 1.0, 0.0, MULT, ADD)
 
         page_q = [held("page_q%d" % c, [P, N], U32) for c in range(chunks)]
@@ -279,21 +280,22 @@ def tile_list_lifeboat_heun_scores_kernel(
         def quantise_page(first, width):
             c, lo = divmod(first, N)
             cols = slice(lo, lo + width)
-            nc.vector.quantize_mx(out=page_q[c][:, cols].bitcast(FP8X4), scales=page_s[c][:, cols], in_=page_bf[c][:, cols, :].rearrange("p n t -> p (n t)"))
+            nc.vector.quantize_mx(out=page_q[c][:, cols].bitcast(FP8X4), scales=page_s[c][:, cols], in_=page_bf[:, first : first + width, :].rearrange("p n t -> p (n t)"))
 
-        round_last(nc.scalar.copy, 2 * N + Q, N + Q)
+        round_last(nc.scalar.copy, 3 * N - P, N + P)
         pair_write(nc.scalar.copy, 3 * N, N)
-        pair_write(nc.scalar.copy, 2 * N + Q, Q)
+        pair_write(nc.scalar.copy, 3 * N - P, P)
         round_last(nc.vector.tensor_copy, 0, N)
-        round_last(nc.vector.tensor_copy, N, N + Q)
+        round_last(nc.vector.tensor_copy, N, 2 * N - P)
         pair_write(nc.vector.tensor_copy, 0, N)
         pair_write(nc.vector.tensor_copy, N, N)
         quantise_page(0, N)
-        pair_write(nc.vector.tensor_copy, 2 * N, Q)
+        pair_write(nc.vector.tensor_copy, 2 * N, N - P)
         quantise_page(N, N)
         quantise_page(2 * N, Q)
         quantise_page(3 * N, N)
-        quantise_page(2 * N + Q, Q)
+        quantise_page(3 * N - P, P)
+        quantise_page(2 * N + Q, P)
 
         def score(b, scores, n, first, width, copy):
             acc = bank(b)
@@ -311,11 +313,12 @@ def tile_list_lifeboat_heun_scores_kernel(
                 score(1, scores, n, N, N, nc.scalar.copy)
                 score(4, scores, n, 2 * N, Q, nc.scalar.copy)
                 score(2, scores, n, 3 * N, N, nc.scalar.copy)
-                score(3, scores, n, 2 * N + Q, Q, nc.vector.tensor_copy)
+                score(5, scores, n, 3 * N - P, P, nc.scalar.copy)
+                score(3, scores, n, 2 * N + Q, P, nc.vector.tensor_copy)
             else:
                 for b, c in ((0, 3), (2, 0), (3, 1), (1, 2)):
                     score(b, scores, n, c * N, N, nc.scalar.copy)
-            pieces = [(0, PICK)] if n < boats - 1 else [(0, N), (N, Q), (N + Q, Q)]
+            pieces = [(0, PICK)] if n < boats - 1 else [(0, N), (N, N - P), (PICK - P, P)]
             for first, width in pieces:
                 picked = held(("t1_0", "t1_1", "flat")[n] if n < boats - 1 else "picked%d" % first, [P, width], F32)
                 nc.vector.tensor_tensor(picked[:], scores[:].indirect(columns(list4, first, width)), reach_sb[n][:, first : first + width], MULT)

@@ -1,6 +1,7 @@
 from contextlib import ExitStack
 
 import concourse.mybir as mybir
+from concourse.masks import make_identity
 
 K, T, S, H, T2, S2, T3, PICK = 512, 4096, 1024, 512, 2048, 512, 2048, 1024
 FLOPS = 2 * (5 * K * H * S + H * S2 * T2)
@@ -77,6 +78,9 @@ def tile_list_lifeboat_heun_scores_kernel(
         nc.vector.memset(wf_s_raw[:].bitcast(I32), 0)
         nc.vector.memset(tab2_s[:].bitcast(I32), 0)
 
+        identity = held("identity", [P, P], F32)
+        make_identity(nc, identity[:])
+
         page_rows = page0.rearrange("(p t) c -> t p c", t=PACK)
         wgs_rows = wgs.rearrange("(m u e) j -> u m e j", u=2, e=2)
 
@@ -101,8 +105,8 @@ def tile_list_lifeboat_heun_scores_kernel(
         nc.sync.dma_start(out=pages[2][:], in_=page_rows[2])
         nc.sync.dma_start(out=tab2_w[:], in_=words_of(tab2_words))
         load_wgs(0, 1)
-        nc.sync.dma_start(out=pages[3][:], in_=page_rows[3])
         load_wgs(1, 1)
+        nc.sync.dma_start(out=pages[3][:], in_=page_rows[3])
         nc.sync.dma_start(list4[:], offs4)
         for n in range(boats):
             nc.sync.dma_start(out=reach_sb[n][:], in_=reach[n * P : (n + 1) * P, :])
@@ -183,10 +187,10 @@ def tile_list_lifeboat_heun_scores_kernel(
                 term[t, h, first] = held("term%d_%d_%d" % (t, h, first), [P, width], F32)[:]
             nc.scalar.activation(term[t, h, first], z2[t, h, first][:, :width], TANH)
 
-        def put(t, h, first, width):
+        def put(t, h, first, width, sum_tile="both"):
             cols = slice(first, first + width)
             values = term[t, h, first]
-            both = held("both", [P, width], F32)
+            both = held(sum_tile, [P, width], F32)
             nc.gpsimd.tensor_tensor(both[:], values, t1[h][:, t, cols], ADD)
             nc.gpsimd.tensor_tensor(values, both[:], weights_of(t, h)[:, cols], MULT)
             nc.vector.tensor_copy(pages[t][:].indirect(columns(list3, h * N + first, width)), values)
@@ -223,16 +227,33 @@ def tile_list_lifeboat_heun_scores_kernel(
             open_second(6 + t, t, 0, Q, Q)
         for t in range(2):
             second_slope(t, 0, Q, Q)
-        for t in range(PACK):
-            z1 = bank(t)
-            state_passes(z1[:], t, 1, 0, N, True)
-            nc.scalar.activation(t1[1][:, t, :], z1[:], TANH)
+        blocks = N // P
+
+        def turned_pass(acc, codes, scales, b, fmt, weights, weight_scales, start, stop):
+            nc.tensor.matmul_mx(
+                out=acc, lhsT=codes[:, b * P : (b + 1) * P].bitcast(FP8X4), lhsT_scale=scales[:, b * P : (b + 1) * P],
+                rhs=weights.bitcast(fmt), rhs_scale=weight_scales, start=start, stop=stop,
+            )
+
+        for b in range(blocks):
+            z1 = bank(b)
+            turned_pass(z1[:], v_w[1], v_s[1], b, FP8X4, wq[:], wq_s[:], True, False)
+            turned_pass(z1[:], v_w[1], v_s[1], b, FP4X4, wf[:], wf_s[:], False, True)
+            nc.scalar.activation(t1[1][:, b, :], z1[:], TANH)
         for t in range(2):
             for first in (0, Q):
                 put(t, 0, first, Q)
         flat = held("flat", [P, PACK, N], BF16)
-        for t in range(PACK):
-            nc.scalar.activation(flat[:, t, :], t1[1][:, t, :], COPY, scale=gain_sb[:, t : t + 1])
+        for q in range(2):
+            for u in range(2):
+                back = bank(2 * q + u)
+                for e in range(2):
+                    for b in range(2):
+                        t = 2 * u + e
+                        nc.tensor.transpose(back[:, e * Q + b * P : e * Q + (b + 1) * P], t1[1][:, 2 * q + b, t * P : (t + 1) * P], identity[:])
+                for e in range(2):
+                    t = 2 * u + e
+                    nc.scalar.activation(flat[:, t, q * Q : (q + 1) * Q], back[:, e * Q : (e + 1) * Q], COPY, scale=gain_sb[:, t : t + 1])
         open_second(4, 2, 0, 0, N)
         second_slope(2, 0, 0, N)
         woven2 = held("woven2", [P, N, PACK], BF16)
@@ -243,25 +264,41 @@ def tile_list_lifeboat_heun_scores_kernel(
         nc.vector.tensor_copy(out=v2_w[:], in_=tab2_w[:].bitcast(U32).indirect(list2[:]))
         scale_weights_scalar(2, 0, "late_terms")
         put(2, 0, 0, N)
-        for t, h in [(0, 1), (1, 1), (3, 0)]:
-            scale_weights_scalar(t, h, "late_terms")
-        late_terms = held("late_terms", [P, 5, N], F32)
-        for i, (t, h) in enumerate([(0, 1), (1, 1), (2, 1), (3, 0), (3, 1)]):
-            term[t, h, 0] = late_terms[:, i, :]
-        term[0, 1, 0], term[0, 1, Q] = late_terms[:, 0, :Q], late_terms[:, 0, Q:]
-        for b, first in [(5, 0), (6, Q)]:
-            open_second(b, 0, 1, first, Q)
-            second_slope(0, 1, first, Q)
-            put(0, 1, first, Q)
-        for b, t, h in [(0, 1, 1), (2, 3, 0), (1, 2, 1), (3, 3, 1)]:
-            open_second(b, t, h, 0, N)
-            if (t // 2, h) == (1, 1):
-                scale_weights_scalar(t, h, "page_bf")
-            second_slope(t, h, 0, N)
-            put(t, h, 0, N)
+        scale_weights_scalar(3, 0, "late_terms")
+        late_terms = held("late_terms", [P, PACK + 1, N], F32)
+
+        def turned_piece(t, z_bank, sum_bank):
+            z = bank(z_bank)
+            plane = slice(t * P, (t + 1) * P)
+            for b in range(blocks):
+                cols = slice(b * P, (b + 1) * P)
+                turned_pass(z[:, cols], v_w[1], v_s[1], b, FP8X4, wq[:, plane], wq_s[:, plane], b == 0, False)
+                turned_pass(z[:, cols], v_w[1], v_s[1], b, FP4X4, wf[:, 2 * t * P : 2 * (t + 1) * P], wf_s[:, plane], False, False)
+            for b in range(blocks):
+                turned_pass(z[:, b * P : (b + 1) * P], d1[1], d1_s[1], b, FP8X4, wq[:, plane], wq_s[:, plane], False, b == blocks - 1)
+            values = late_terms[:, t, :]
+            nc.scalar.activation(values, z[:], TANH)
+            total = bank(sum_bank)
+            for b in range(blocks):
+                nc.tensor.matmul(total[:, b * P : (b + 1) * P], t1[1][:, b, plane], identity[:], start=b == 0, stop=False, is_transpose=True)
+            for b in range(blocks):
+                cols = slice(b * P, (b + 1) * P)
+                nc.tensor.matmul(total[:, cols], values[:, cols], identity[:], start=False, stop=b == blocks - 1, is_transpose=True)
+            nc.scalar.activation(values, total[:], COPY, scale=half_gain["page_bf"][:, t : t + 1])
+            nc.gpsimd.tensor_tensor(values, values, weights_of(t, 1), MULT)
+            nc.vector.tensor_copy(pages[t][:].indirect(columns(list3, N, N)), values)
+
+        turned_piece(0, 5, 0)
+        turned_piece(1, 2, 1)
+        turned_piece(2, 3, 6)
+        term[3, 0, 0] = late_terms[:, PACK, :]
+        open_second(1, 3, 0, 0, N)
+        second_slope(3, 0, 0, N)
+        put(3, 0, 0, N, "wgs01")
+        turned_piece(3, 5, 1)
 
         page_bf = held("page_bf", [P, T2, PACK], BF16)
-        rounded = held("both", [P, 2, T2], BF16)
+        rounded = held("wgs11", [P, 2, T2], BF16)
 
         def pair_write(copy, first, width):
             copy(out=page_bf[:, first : first + width, 2:], in_=rounded[:, :, first : first + width].rearrange("p e n -> p n e"))

@@ -200,8 +200,8 @@ def tile_list_lifeboat_heun_scores_kernel(
             nc.vector.quantize_mx(out=d1[h][:, cols].bitcast(FP8X4), scales=d1_s[h][:, cols], in_=woven[:].rearrange("p n t -> p (n t)"))
 
         warm = bank(7)
-        for i in range(5):
-            pass_w(warm[:], 0, wq[:], wq_s[:], True, True)
+        for i in range(3):
+            pass_w(warm[:], 0, wq[:], v_s[1][:], True, True)
         for t in range(2):
             scale_weights_gpsimd(t, 0, "both")
         woven0 = held("woven0", [P, Q, PACK], BF16)
@@ -221,7 +221,10 @@ def tile_list_lifeboat_heun_scores_kernel(
         for t in range(2):
             second_slope(t, 0, 0, Q)
         woven1 = held("woven1", [P, Q, PACK], BF16)
-        nc.vector.tensor_tensor(woven1[:], t1[0][:, :, Q:].rearrange("p t n -> p n t"), gain_sb[:].unsqueeze(1).to_broadcast([P, Q, PACK]), MULT)
+        nc.vector.tensor_tensor(
+            woven1[:].rearrange("p (c i) t -> p c t i", i=4), t1[0][:, :, Q:].rearrange("p t (c i) -> p c t i", i=4),
+            gain_sb[:].unsqueeze(1).unsqueeze(3).to_broadcast([P, Q // 4, PACK, 4]), MULT,
+        )
         quantise_d1(0, Q, Q, woven1)
         for t in range(2):
             open_second(6 + t, t, 0, Q, Q)
@@ -267,38 +270,41 @@ def tile_list_lifeboat_heun_scores_kernel(
         scale_weights_scalar(3, 0, "late_terms")
         late_terms = held("late_terms", [P, PACK + 1, N], F32)
 
-        def turned_piece(t, z_bank, sum_bank):
+        def turned_piece(t, z_bank, sum_bank, first=0, width=N):
             z = bank(z_bank)
             plane = slice(t * P, (t + 1) * P)
-            for b in range(blocks):
-                cols = slice(b * P, (b + 1) * P)
-                turned_pass(z[:, cols], v_w[1], v_s[1], b, FP8X4, wq[:, plane], wq_s[:, plane], b == 0, False)
+            here = [(first // P + b, slice(b * P, (b + 1) * P)) for b in range(width // P)]
+            last = here[-1][0]
+            for b, cols in here:
+                turned_pass(z[:, cols], v_w[1], v_s[1], b, FP8X4, wq[:, plane], wq_s[:, plane], b == here[0][0], False)
                 turned_pass(z[:, cols], v_w[1], v_s[1], b, FP4X4, wf[:, 2 * t * P : 2 * (t + 1) * P], wf_s[:, plane], False, False)
-            for b in range(blocks):
-                turned_pass(z[:, b * P : (b + 1) * P], d1[1], d1_s[1], b, FP8X4, wq[:, plane], wq_s[:, plane], False, b == blocks - 1)
-            values = late_terms[:, t, :]
-            nc.scalar.activation(values, z[:], TANH)
+            for b, cols in here:
+                turned_pass(z[:, cols], d1[1], d1_s[1], b, FP8X4, wq[:, plane], wq_s[:, plane], False, b == last)
+            values = late_terms[:, t, first : first + width]
+            nc.scalar.activation(values, z[:, :width], TANH)
             total = bank(sum_bank)
-            for b in range(blocks):
-                nc.tensor.matmul(total[:, b * P : (b + 1) * P], t1[1][:, b, plane], identity[:], start=b == 0, stop=False, is_transpose=True)
-            for b in range(blocks):
-                cols = slice(b * P, (b + 1) * P)
-                nc.tensor.matmul(total[:, cols], values[:, cols], identity[:], start=False, stop=b == blocks - 1, is_transpose=True)
-            nc.scalar.activation(values, total[:], COPY, scale=half_gain["page_bf"][:, t : t + 1])
-            nc.gpsimd.tensor_tensor(values, values, weights_of(t, 1), MULT)
-            nc.vector.tensor_copy(pages[t][:].indirect(columns(list3, N, N)), values)
+            for b, cols in here:
+                nc.tensor.matmul(total[:, cols], t1[1][:, b, plane], identity[:], start=b == here[0][0], stop=False, is_transpose=True)
+            for b, cols in here:
+                nc.tensor.matmul(total[:, cols], values[:, cols], identity[:], start=False, stop=b == last, is_transpose=True)
+            nc.scalar.activation(values, total[:, :width], COPY, scale=half_gain["page_bf"][:, t : t + 1])
+            nc.gpsimd.tensor_tensor(values, values, weights_of(t, 1)[:, first : first + width], MULT)
+            nc.vector.tensor_copy(pages[t][:].indirect(columns(list3, N + first, width)), values)
 
-        turned_piece(0, 5, 0)
+        turned_piece(0, 5, 0, 0, Q)
+        turned_piece(0, 7, 4, Q, Q)
         turned_piece(1, 2, 1)
         turned_piece(2, 3, 6)
         term[3, 0, 0] = late_terms[:, PACK, :]
-        open_second(1, 3, 0, 0, N)
+        open_second(0, 3, 0, 0, N)
         second_slope(3, 0, 0, N)
         put(3, 0, 0, N, "wgs01")
-        turned_piece(3, 5, 1)
+        turned_piece(3, 5, 0)
 
         page_bf = held("page_bf", [P, T2, PACK], BF16)
         rounded = held("wgs11", [P, 2, T2], BF16)
+        one = held("wgs10", [P, 1], F32)
+        nc.gpsimd.memset(one[:], 1.0)
 
         def pair_write(copy, first, width):
             copy(out=page_bf[:, first : first + width, 2:], in_=rounded[:, :, first : first + width].rearrange("p e n -> p n e"))
@@ -306,7 +312,10 @@ def tile_list_lifeboat_heun_scores_kernel(
         for t in range(2):
             for c in range(chunks):
                 nc.scalar.copy(out=page_bf[:, c * N : (c + 1) * N, t], in_=pages[t][:, c * N : (c + 1) * N])
-        nc.gpsimd.tensor_scalar(rounded[:, 0, :], pages[2][:], 1.0, 0.0, MULT, ADD)
+        for c in range(2):
+            cols = slice(c * N, (c + 1) * N)
+            nc.gpsimd.tensor_scalar(page_bf[:, cols, 2:], pages[2][:, cols].unsqueeze(2).to_broadcast([P, N, 2]), one[:], 0.0, MULT, ADD)
+        nc.gpsimd.tensor_scalar(rounded[:, 0, 2 * N :], pages[2][:, 2 * N :], 1.0, 0.0, MULT, ADD)
 
         page_q = [held("page_q%d" % c, [P, N], U32) for c in range(chunks)]
         page_s = [held("page_s%d" % c, [P, N], U8) for c in range(chunks)]
@@ -322,10 +331,9 @@ def tile_list_lifeboat_heun_scores_kernel(
         round_last(nc.scalar.copy, 3 * N - P, N + P)
         pair_write(nc.scalar.copy, 3 * N, N)
         pair_write(nc.scalar.copy, 3 * N - P, P)
-        round_last(nc.vector.tensor_copy, 0, N)
-        round_last(nc.vector.tensor_copy, N, 2 * N - P)
-        pair_write(nc.vector.tensor_copy, 0, N)
-        pair_write(nc.vector.tensor_copy, N, N)
+        for c in range(2):
+            nc.vector.tensor_copy(out=page_bf[:, c * N : (c + 1) * N, 3], in_=pages[3][:, c * N : (c + 1) * N])
+        round_last(nc.vector.tensor_copy, 2 * N, N - P)
         quantise_page(0, N)
         pair_write(nc.vector.tensor_copy, 2 * N, N - P)
         quantise_page(N, N)

@@ -191,8 +191,8 @@ def tile_list_lifeboat_heun_scores_kernel(
             cols = slice(first, first + width)
             values = term[t, h, first]
             both = held(sum_tile, [P, width], F32)
-            nc.gpsimd.tensor_tensor(both[:], values, t1[h][:, t, cols], ADD)
-            nc.gpsimd.tensor_tensor(values, both[:], weights_of(t, h)[:, cols], MULT)
+            nc.vector.tensor_tensor(both[:], values, t1[h][:, t, cols], ADD)
+            nc.vector.tensor_tensor(values, both[:], weights_of(t, h)[:, cols], MULT)
             nc.vector.tensor_copy(pages[t][:].indirect(columns(list3, h * N + first, width)), values)
 
         def quantise_d1(h, first, width, woven):
@@ -288,7 +288,7 @@ def tile_list_lifeboat_heun_scores_kernel(
             for b, cols in here:
                 nc.tensor.matmul(total[:, cols], values[:, cols], identity[:], start=False, stop=b == last, is_transpose=True)
             nc.scalar.activation(values, total[:, :width], COPY, scale=half_gain["page_bf"][:, t : t + 1])
-            nc.gpsimd.tensor_tensor(values, values, weights_of(t, 1)[:, first : first + width], MULT)
+            nc.vector.tensor_tensor(values, values, weights_of(t, 1)[:, first : first + width], MULT)
             nc.vector.tensor_copy(pages[t][:].indirect(columns(list3, N + first, width)), values)
 
         turned_piece(0, 5, 0, 0, Q)

@@ -32,7 +32,6 @@ def tile_list_lifeboat_heun_scores_kernel(
 ):
     nc = tc.nc
     halves = S // N
-    chunks = T2 // N
     boats = S2 // P
 
     with ExitStack() as ctx:
@@ -45,9 +44,9 @@ def tile_list_lifeboat_heun_scores_kernel(
         def bank(b):
             return psum.tile([P, N], F32, name="bank%d" % b)
 
-        def load_scale_rows(plane, rows, queue=nc.sync):
+        def load_scale_rows(plane, rows):
             for q in range(4):
-                queue.dma_start(
+                nc.sync.dma_start(
                     out=plane[32 * q : 32 * q + 4, :].bitcast(I32),
                     in_=rows[0, 4 * q : 4 * q + 4, :].bitcast(I32),
                 )
@@ -66,15 +65,17 @@ def tile_list_lifeboat_heun_scores_kernel(
         tab_s = held("tab_s", [P, T], U8)
         tab2_w = held("tab2_w", [P, T3], I32)
         tab2_s = held("tab2_s", [P, T3], U8)
-        w_raw = held("w_raw", [P, PACK, H], F32)
+        w_raw = [held("w_raw%d" % u, [P, PACK, Q], F32) for u in range(2)]
         wf_raw = held("wf_raw", [P, 2 * H], U8)
         wf_s_raw = held("wf_s_raw", [P, H], U8)
         gain_sb = held("gain_sb", [P, PACK], F32)
         pages = [held("page%d" % t, [P, T2], F32) for t in range(PACK)]
-        wgs_sb = {(u, h): held("wgs%d%d" % (u, h), [P, 2, N], F32) for u in range(2) for h in range(halves)}
+        wgs_cuts = [(0, Q), (Q, Q), (N, N)]
+        wgs_sb = {first: held("wgs%d" % first, [P, PACK, width], F32) for first, width in wgs_cuts}
         reach_sb = [held("reach%d" % n, [P, PICK], F32) for n in range(boats)]
 
-        nc.vector.memset(tab_s[:].bitcast(I32), 0)
+        nc.gpsimd.memset(tab_s[:, : T // 2].bitcast(I32), 0)
+        nc.vector.memset(tab_s[:, T // 2 :].bitcast(I32), 0)
         nc.vector.memset(wf_s_raw[:].bitcast(I32), 0)
         nc.vector.memset(tab2_s[:].bitcast(I32), 0)
 
@@ -82,289 +83,331 @@ def tile_list_lifeboat_heun_scores_kernel(
         make_identity(nc, identity[:])
 
         page_rows = page0.rearrange("(p t) c -> t p c", t=PACK)
-        wgs_rows = wgs.rearrange("(m u e) j -> u m e j", u=2, e=2)
+        wgs_rows = wgs.rearrange("(m t) j -> m t j", t=PACK)
+        w_rows = w.rearrange("(p j) c -> p j c", j=PACK)
 
-        def load_wgs(u, h):
+        def load_wgs(first, width):
             for q in (0, 2, 1, 3):
-                nc.sync.dma_start(out=wgs_sb[u, h][32 * q : 32 * q + 32], in_=wgs_rows[u, :, :, h * N : (h + 1) * N])
+                nc.sync.dma_start(out=wgs_sb[first][32 * q : 32 * q + 32], in_=wgs_rows[:, :, first : first + width])
 
-        nc.sync.dma_start(out=w_raw[:], in_=w.rearrange("(p j) c -> p j c", j=PACK))
         nc.sync.dma_start(list1[:], offs)
-        load_scale_rows(tab_s, tab_scales)
+        nc.sync.dma_start(out=gain_sb[:], in_=gain.rearrange("(p t) -> p t", t=PACK))
         nc.sync.dma_start(out=wf_raw[:].bitcast(I32), in_=wf_words[0].bitcast(I32))
+        load_scale_rows(tab_s, tab_scales)
         nc.sync.dma_start(out=tab_w[:], in_=words_of(tab_words))
         load_scale_rows(wf_s_raw, wf_scales)
-        nc.sync.dma_start(out=gain_sb[:], in_=gain.rearrange("(p t) -> p t", t=PACK))
-        load_wgs(0, 0)
+        for u in range(2):
+            nc.sync.dma_start(out=w_raw[u][:], in_=w_rows[:, :, u * Q : (u + 1) * Q])
         nc.sync.dma_start(list2[:], offs2)
         load_scale_rows(tab2_s, tab2_scales)
+        load_wgs(*wgs_cuts[0])
         nc.sync.dma_start(list3[:], offs3)
-        nc.sync.dma_start(out=pages[0][:], in_=page_rows[0])
-        nc.sync.dma_start(out=pages[1][:], in_=page_rows[1])
-        load_wgs(1, 0)
-        nc.sync.dma_start(out=pages[2][:], in_=page_rows[2])
+        for t in range(PACK):
+            nc.sync.dma_start(out=pages[t][:], in_=page_rows[t])
+        load_wgs(*wgs_cuts[1])
+        load_wgs(*wgs_cuts[2])
         nc.sync.dma_start(out=tab2_w[:], in_=words_of(tab2_words))
-        load_wgs(0, 1)
-        load_wgs(1, 1)
-        nc.sync.dma_start(out=pages[3][:], in_=page_rows[3])
         nc.sync.dma_start(list4[:], offs4)
         for n in range(boats):
             nc.sync.dma_start(out=reach_sb[n][:], in_=reach[n * P : (n + 1) * P, :])
 
-        w_bf = [held("w_bf%d" % u, [P, 2 * H], BF16) for u in range(2)]
-        wq = held("wq", [P, H], U32)
-        wq_s = held("wq_s", [P, H], U8)
-        w_in = w_raw[:].rearrange("p j (m t) -> p t m j", t=PACK)
-        nc.vector.tensor_copy(out=w_bf[0][:].rearrange("p (t m j) -> p m t j", t=2, j=PACK), in_=w_in[:, :2].rearrange("p t m j -> p m t j"))
-        nc.scalar.copy(out=w_bf[1][:].rearrange("p (t m j) -> p t m j", t=2, j=PACK), in_=w_in[:, 2:])
         v_w = [held("v_w%d" % h, [P, N], U32) for h in range(halves)]
         v_s = [held("v_s%d" % h, [P, N], U8) for h in range(halves)]
-        nc.vector.tensor_copy(out=v_s[0][:], in_=tab_s[:].indirect(columns(list1, 0, N)))
-        for u in range(2):
-            cols = slice(u * H // 2, (u + 1) * H // 2)
-            nc.vector.quantize_mx(out=wq[:, cols].bitcast(FP8X4), scales=wq_s[:, cols], in_=w_bf[u][:])
         wf = held("wf", [P, 2 * H], U8)
         wf_s = held("wf_s", [P, H], U8)
         nc.vector.tensor_copy(
             out=wf[:].bitcast(U16).rearrange("p (t m) -> p t m", t=PACK),
             in_=wf_raw[:].bitcast(U16).rearrange("p (m t) -> p t m", t=PACK),
         )
-        nc.vector.tensor_copy(out=v_s[1][:], in_=tab_s[:].indirect(columns(list1, N, N)))
-        nc.vector.tensor_copy(out=v_w[0][:], in_=tab_w[:].bitcast(U32).indirect(columns(list1, 0, N)))
-        nc.vector.tensor_copy(
+        for h in range(halves):
+            nc.vector.tensor_copy(out=v_s[h][:], in_=tab_s[:].indirect(columns(list1, h * N, N)))
+        for h in range(halves):
+            nc.vector.tensor_copy(out=v_w[h][:], in_=tab_w[:].bitcast(U32).indirect(columns(list1, h * N, N)))
+        nc.gpsimd.tensor_copy(
             out=wf_s[:].rearrange("p (t m) -> p t m", t=PACK),
             in_=wf_s_raw[:].rearrange("p (m t) -> p t m", t=PACK),
         )
-        half_gain = {}
-        for name in ("both", "late_terms", "page_bf"):
-            half_gain[name] = held(name, [P, PACK], F32)
-            nc.vector.tensor_scalar(half_gain[name][:], gain_sb[:], 0.5, None, MULT)
-        nc.vector.tensor_copy(out=v_w[1][:], in_=tab_w[:].bitcast(U32).indirect(columns(list1, N, N)))
+
+        w_bf = [held("w_bf%d" % u, [P, 2, P, PACK], BF16) for u in range(2)]
+        wq = held("wq", [P, H], U32)
+        wq_s = held("wq_s", [P, H], U8)
+
+        def round_w(copy, part, u):
+            half = slice(part * P // 2, (part + 1) * P // 2)
+            copy(
+                out=w_bf[u][:, :, half, :].rearrange("p t m j -> p m t j"),
+                in_=w_raw[part][:].rearrange("p j (m t) -> p m t j", t=PACK)[:, :, 2 * u : 2 * u + 2, :],
+            )
+
+        def quantise_w(u):
+            cols = slice(u * Q, (u + 1) * Q)
+            nc.vector.quantize_mx(out=wq[:, cols].bitcast(FP8X4), scales=wq_s[:, cols], in_=w_bf[u][:].rearrange("p t m j -> p (t m j)"))
+
+        for u in range(2):
+            round_w(nc.scalar.copy, 0, u)
+        round_w(nc.vector.tensor_copy, 1, 0)
+        round_w(nc.scalar.copy, 1, 1)
+        for u in range(2):
+            quantise_w(u)
+        half_gain = held("half_gain", [P, PACK], F32)
+        nc.gpsimd.tensor_scalar(half_gain[:], gain_sb[:], 0.5, 0.0, MULT, ADD)
+        early_gain = {}
+        for t, name in ((2, "t2_2"), (3, "t1_4")):
+            early_gain[t] = held(name, [P, 1], F32)
+            nc.gpsimd.tensor_scalar(early_gain[t][:], gain_sb[:, t : t + 1], 0.5, 0.0, MULT, ADD)
         v2_s = held("v2_s", [P, S2], U8)
         nc.vector.tensor_copy(out=v2_s[:], in_=tab2_s[:].indirect(list2[:]))
 
-        def pass_w(acc, t, codes, scales, start, stop):
+        def entries(b):
+            h, lo = divmod(b * P, N)
+            return v_w[h][:, lo : lo + P], v_s[h][:, lo : lo + P]
+
+        def mx(acc, left, fmt, codes, scales, start, stop):
             nc.tensor.matmul_mx(
-                out=acc, lhsT=wq[:, t * P : (t + 1) * P].bitcast(FP8X4), lhsT_scale=wq_s[:, t * P : (t + 1) * P],
+                out=acc, lhsT=left[0].bitcast(FP8X4), lhsT_scale=left[1],
+                rhs=codes.bitcast(fmt), rhs_scale=scales, start=start, stop=stop,
+            )
+
+        def forcing_pass(acc, b):
+            mx(acc[:], entries(b), FP4X4, wf[:], wf_s[:], True, False)
+
+        def drift_pass(acc, left, stop, first=0, width=N):
+            cols = slice(first, first + width)
+            mx(acc[:, cols], left, FP8X4, wq[:, cols], wq_s[:, cols], False, stop)
+
+        blocks = S // P
+        t1 = {b: held("t1_%d" % b, [P, PACK, P], F32) for b in range(2, blocks) if b != 4}
+        t2 = {b: held("t2_%d" % b, [P, PACK, P], F32) for b in range(3, blocks)}
+        woven = {q: held("woven%d" % q, [P, Q, PACK], BF16) for q in range(3)}
+        d1 = {q: held("d1_%d" % q, [P, Q], U32) for q in (0, 1, 3)}
+        d1_s = [held("d1_s%d" % q, [P, Q], U8) for q in range(S // Q)]
+        z2 = {}
+
+        def by_plane(acc):
+            return acc[:].rearrange("p (t m) -> p t m", t=PACK)
+
+        def first_slope(b):
+            z1 = bank(b % 2)
+            forcing_pass(z1, b)
+            drift_pass(z1, entries(b), True)
+            nc.scalar.activation(t1[b][:], by_plane(z1), TANH)
+
+        def first_step(b):
+            back = bank(2 + b % 2)
+            for t in range(PACK):
+                nc.tensor.transpose(back[:, t * P : (t + 1) * P], t1[b][:, t, :], identity[:])
+            q, lo = divmod(b * P, Q)
+            nc.vector.tensor_tensor(
+                woven[q][:, lo : lo + P, :], back[:].rearrange("p (t n) -> p n t", t=PACK),
+                gain_sb[:].unsqueeze(1).to_broadcast([P, P, PACK]), MULT,
+            )
+
+        def quantise_step(q, lo=0, width=Q):
+            cols = slice(lo, lo + width)
+            nc.vector.quantize_mx(out=d1[q][:, cols].bitcast(FP8X4), scales=d1_s[q][:, cols], in_=woven[q][:, cols, :].rearrange("p n t -> p (n t)"))
+
+        def open_second(b):
+            z2[b] = bank(4 + b % 2)
+            forcing_pass(z2[b], b)
+            drift_pass(z2[b], entries(b), False)
+
+        def close_second(b):
+            q, lo = divmod(b * P, Q)
+            drift_pass(z2[b], (d1[q][:, lo : lo + P], d1_s[q][:, lo : lo + P]), True)
+
+        def second_slope(b, planes=slice(0, PACK)):
+            nc.scalar.activation(t2[b][:, planes, :], by_plane(z2[b])[:, planes, :], TANH)
+
+        def slope_sum(sum_bank, t, first, width):
+            total = bank(sum_bank)
+            here = range(first // P, (first + width) // P)
+            for k, slopes in enumerate((t1, t2)):
+                for b in here:
+                    lo = b * P - first
+                    nc.tensor.matmul(
+                        total[:, lo : lo + P], slopes[b][:, t, :], identity[:],
+                        start=k == 0 and b == here[0], stop=k == 1 and b == here[-1], is_transpose=True,
+                    )
+            return total[:, :width]
+
+        def weights_of(t, first, width):
+            base = min(first, N)
+            return wgs_sb[base][:, t, first - base : first - base + width]
+
+        def make_values(values, sum_bank, t, first, width, staged=None):
+            staged = values if staged is None else staged
+            nc.scalar.activation(staged, slope_sum(sum_bank, t, first, width), COPY, scale=half_gain[:, t : t + 1])
+            nc.gpsimd.tensor_tensor(values, staged, weights_of(t, first, width), MULT)
+
+        def put(values, t, first, width):
+            nc.vector.tensor_copy(pages[t][:].indirect(columns(list3, first, width)), values)
+
+        def piece(sum_bank, t, first, width):
+            values = held("values%d_%d" % (t, first), [P, width], F32)
+            make_values(values[:], sum_bank, t, first, width)
+            put(values[:], t, first, width)
+
+        def upright(acc, t, fmt, codes, scales, start, stop):
+            size = 2 if fmt == FP4X4 else 1
+            weights, weight_scales = (wf, wf_s) if fmt == FP4X4 else (wq, wq_s)
+            nc.tensor.matmul_mx(
+                out=acc, lhsT=weights[:, size * t * P : size * (t + 1) * P].bitcast(fmt), lhsT_scale=weight_scales[:, t * P : (t + 1) * P],
                 rhs=codes.bitcast(FP8X4), rhs_scale=scales, start=start, stop=stop,
             )
 
-        def state_passes(acc, t, h, first, width, stop):
-            pass_w(acc, t, v_w[h][:, first : first + width], v_s[h][:, first : first + width], True, False)
-            piece = N if width == N else P
-            for lo in range(0, width, piece):
-                cols = slice(first + lo, first + lo + piece)
-                nc.tensor.matmul_mx(
-                    out=acc[:, lo : lo + piece],
-                    lhsT=wf[:, 2 * t * P : 2 * (t + 1) * P].bitcast(FP4X4), lhsT_scale=wf_s[:, t * P : (t + 1) * P],
-                    rhs=v_w[h][:, cols].bitcast(FP8X4), rhs_scale=v_s[h][:, cols],
-                    start=False, stop=stop and lo + piece == width,
-                )
-
-        t1 = [held("t1_%d" % h, [P, PACK, N], F32) for h in range(halves)]
-        d1 = [held("d1_0", [P, N], U32)]
-        d1_s = [held("d1_s%d" % h, [P, N], U8) for h in range(halves)]
-        z2 = {}
-        term = {}
-
-        def weights_of(t, h):
-            return wgs_sb[t // 2, h][:, t % 2, :]
-
-        def scale_weights_gpsimd(t, h, name):
-            nc.gpsimd.tensor_scalar(weights_of(t, h), weights_of(t, h), half_gain[name][:, t : t + 1], 0.0, MULT, ADD)
-
-        def scale_weights_scalar(t, h, name):
-            nc.scalar.activation(weights_of(t, h), weights_of(t, h), COPY, scale=half_gain[name][:, t : t + 1])
-
-        def open_second(b, t, h, first, width):
-            z2[t, h, first] = bank(b)
-            state_passes(z2[t, h, first][:, :width], t, h, first, width, False)
-
-        def second_slope(t, h, first, width):
-            cols = slice(first, first + width)
-            pass_w(z2[t, h, first][:, :width], t, d1[h][:, cols], d1_s[h][:, cols], False, True)
-            if (t, h, first) not in term:
-                term[t, h, first] = held("term%d_%d_%d" % (t, h, first), [P, width], F32)[:]
-            nc.scalar.activation(term[t, h, first], z2[t, h, first][:, :width], TANH)
-
-        def put(t, h, first, width, sum_tile="both"):
-            cols = slice(first, first + width)
-            values = term[t, h, first]
-            both = held(sum_tile, [P, width], F32)
-            nc.vector.tensor_tensor(both[:], values, t1[h][:, t, cols], ADD)
-            nc.vector.tensor_tensor(values, both[:], weights_of(t, h)[:, cols], MULT)
-            nc.vector.tensor_copy(pages[t][:].indirect(columns(list3, h * N + first, width)), values)
-
-        def quantise_d1(h, first, width, woven):
-            cols = slice(first, first + width)
-            nc.vector.quantize_mx(out=d1[h][:, cols].bitcast(FP8X4), scales=d1_s[h][:, cols], in_=woven[:].rearrange("p n t -> p (n t)"))
-
-        warm = bank(7)
-        for i in range(3):
-            pass_w(warm[:], 0, wq[:], v_s[1][:], True, True)
-        for t in range(2):
-            scale_weights_gpsimd(t, 0, "both")
-        woven0 = held("woven0", [P, Q, PACK], BF16)
-        for t in range(PACK):
-            z1 = bank(t)
-            state_passes(z1[:, :Q], t, 0, 0, Q, True)
-            nc.scalar.activation(t1[0][:, t, :Q], z1[:, :Q], TANH)
-            nc.vector.tensor_scalar(woven0[:, :, t], t1[0][:, t, :Q], gain_sb[:, t : t + 1], None, MULT)
-        quantise_d1(0, 0, Q, woven0)
-        for u in range(2):
-            z1 = bank(6 + u)
-            for e in range(2):
-                state_passes(z1[:, e * Q : (e + 1) * Q], 2 * u + e, 0, Q, Q, True)
-            nc.scalar.activation(t1[0][:, 2 * u : 2 * u + 2, Q:], z1[:].rearrange("p (e n) -> p e n", e=2), TANH)
-        for t in range(2):
-            open_second(4 + t, t, 0, 0, Q)
-        for t in range(2):
-            second_slope(t, 0, 0, Q)
-        woven1 = held("woven1", [P, Q, PACK], BF16)
-        nc.vector.tensor_tensor(
-            woven1[:].rearrange("p (c i) t -> p c t i", i=4), t1[0][:, :, Q:].rearrange("p t (c i) -> p c t i", i=4),
-            gain_sb[:].unsqueeze(1).unsqueeze(3).to_broadcast([P, Q // 4, PACK, 4]), MULT,
-        )
-        quantise_d1(0, Q, Q, woven1)
-        for t in range(2):
-            open_second(6 + t, t, 0, Q, Q)
-        for t in range(2):
-            second_slope(t, 0, Q, Q)
-        blocks = N // P
-
-        def turned_pass(acc, codes, scales, b, fmt, weights, weight_scales, start, stop):
-            nc.tensor.matmul_mx(
-                out=acc, lhsT=codes[:, b * P : (b + 1) * P].bitcast(FP8X4), lhsT_scale=scales[:, b * P : (b + 1) * P],
-                rhs=weights.bitcast(fmt), rhs_scale=weight_scales, start=start, stop=stop,
+        up1 = held("up1", [P, PACK, Q], F32)
+        up2 = held("up2", [P, PACK, Q], F32)
+        early = [bank(b) for b in range(2)]
+        for b in range(2):
+            for t in range(PACK):
+                upright(early[b][:, t * P : (t + 1) * P], t, FP4X4, *entries(b), t == 0, False)
+        for b in range(2):
+            cols = slice(b * P, (b + 1) * P)
+            for t in range(PACK):
+                upright(early[b][:, t * P : (t + 1) * P], t, FP8X4, *entries(b), False, t == PACK - 1)
+            nc.scalar.activation(up1[:, :, cols], by_plane(early[b]), TANH)
+            nc.vector.tensor_tensor(
+                woven[0][:, cols, :].rearrange("p (c i) t -> p c t i", i=4), up1[:, :, cols].rearrange("p t (c i) -> p c t i", i=4),
+                gain_sb[:].unsqueeze(1).unsqueeze(3).to_broadcast([P, P // 4, PACK, 4]), MULT,
             )
+        for b in range(2):
+            quantise_step(0, b * P, P)
 
-        for b in range(blocks):
-            z1 = bank(b)
-            turned_pass(z1[:], v_w[1], v_s[1], b, FP8X4, wq[:], wq_s[:], True, False)
-            turned_pass(z1[:], v_w[1], v_s[1], b, FP4X4, wf[:], wf_s[:], False, True)
-            nc.scalar.activation(t1[1][:, b, :], z1[:], TANH)
+        def upright_second(z_bank, planes):
+            z = bank(z_bank)
+            for e, t in enumerate(planes):
+                for b in range(2):
+                    upright(z[:, e * Q + b * P : e * Q + (b + 1) * P], t, FP4X4, *entries(b), e == 0 and b == 0, False)
+                upright(z[:, e * Q : (e + 1) * Q], t, FP8X4, v_w[0][:, :Q], v_s[0][:, :Q], False, False)
+            for e, t in enumerate(planes):
+                upright(z[:, e * Q : (e + 1) * Q], t, FP8X4, d1[0][:], d1_s[0][:], False, t == planes[-1])
+            rows = slice(planes[0], planes[-1] + 1)
+            nc.scalar.activation(up2[:, rows, :], z[:, : len(planes) * Q].rearrange("p (e n) -> p e n", n=Q), TANH)
+            return rows
+
         for t in range(2):
-            for first in (0, Q):
-                put(t, 0, first, Q)
-        flat = held("flat", [P, PACK, N], BF16)
-        for q in range(2):
+            upright_second(4 + t, [t])
+        both = held("pair", [P, 2, Q], F32)
+        nc.vector.tensor_tensor(both[:], up2[:, :2, :], up1[:, :2, :], ADD)
+        values = [held("values%d_0" % t, [P, Q], F32) for t in range(2)]
+        for t in range(2):
+            nc.vector.scalar_tensor_tensor(values[t][:], both[:, t, :], half_gain[:, t : t + 1], weights_of(t, 0, Q), MULT, MULT)
+        for t in range(2):
+            put(values[t][:], t, 0, Q)
+        for t in (2, 3):
+            nc.scalar.activation(weights_of(t, 0, Q), weights_of(t, 0, Q), COPY, scale=early_gain[t][:])
+        rows = upright_second(6, [2, 3])
+        pair = held("pair", [P, 2, Q], F32)
+        nc.gpsimd.tensor_tensor(pair[:], up2[:, rows, :], up1[:, rows, :], ADD)
+        nc.gpsimd.tensor_tensor(pair[:], pair[:], wgs_sb[0][:, rows, :], MULT)
+        for b in (2, 3):
+            first_slope(b)
+            first_step(b)
+        quantise_step(1)
+        for t in (2, 3):
+            put(pair[:, t - 2, :], t, 0, Q)
+
+        def gpsimd_round(out, in_):
+            nc.gpsimd.tensor_scalar(out, in_, 1.0, 0.0, MULT, ADD)
+
+        def late_step(q):
+            flat = held("flat%d" % q, [P, PACK, Q], BF16)
             for u in range(2):
-                back = bank(2 * q + u)
+                back = bank(2 + u)
                 for e in range(2):
                     for b in range(2):
-                        t = 2 * u + e
-                        nc.tensor.transpose(back[:, e * Q + b * P : e * Q + (b + 1) * P], t1[1][:, 2 * q + b, t * P : (t + 1) * P], identity[:])
+                        nc.tensor.transpose(back[:, e * Q + b * P : e * Q + (b + 1) * P], t1[2 * q + b][:, 2 * u + e, :], identity[:])
                 for e in range(2):
                     t = 2 * u + e
-                    nc.scalar.activation(flat[:, t, q * Q : (q + 1) * Q], back[:, e * Q : (e + 1) * Q], COPY, scale=gain_sb[:, t : t + 1])
-        open_second(4, 2, 0, 0, N)
-        second_slope(2, 0, 0, N)
-        woven2 = held("woven2", [P, N, PACK], BF16)
-        nc.scalar.copy(out=woven2[:].rearrange("p (c i) t -> p c t i", i=4), in_=flat[:].rearrange("p t (c i) -> p c t i", i=4))
-        d1.append(held("term1_0_%d" % Q, [P, N], U32))
-        quantise_d1(1, 0, N, woven2)
-        v2_w = held("woven2", [P, S2], U32)
-        nc.vector.tensor_copy(out=v2_w[:], in_=tab2_w[:].bitcast(U32).indirect(list2[:]))
-        scale_weights_scalar(2, 0, "late_terms")
-        put(2, 0, 0, N)
-        scale_weights_scalar(3, 0, "late_terms")
-        late_terms = held("late_terms", [P, PACK + 1, N], F32)
+                    nc.scalar.activation(flat[:, t, :], back[:, e * Q : (e + 1) * Q], COPY, scale=gain_sb[:, t : t + 1])
+            gpsimd_round(woven[q][:], flat[:].rearrange("p t n -> p n t"))
 
-        def turned_piece(t, z_bank, sum_bank, first=0, width=N):
-            z = bank(z_bank)
-            plane = slice(t * P, (t + 1) * P)
-            here = [(first // P + b, slice(b * P, (b + 1) * P)) for b in range(width // P)]
-            last = here[-1][0]
-            for b, cols in here:
-                turned_pass(z[:, cols], v_w[1], v_s[1], b, FP8X4, wq[:, plane], wq_s[:, plane], b == here[0][0], False)
-                turned_pass(z[:, cols], v_w[1], v_s[1], b, FP4X4, wf[:, 2 * t * P : 2 * (t + 1) * P], wf_s[:, plane], False, False)
-            for b, cols in here:
-                turned_pass(z[:, cols], d1[1], d1_s[1], b, FP8X4, wq[:, plane], wq_s[:, plane], False, b == last)
-            values = late_terms[:, t, first : first + width]
-            nc.scalar.activation(values, z[:, :width], TANH)
-            total = bank(sum_bank)
-            for b, cols in here:
-                nc.tensor.matmul(total[:, cols], t1[1][:, b, plane], identity[:], start=b == here[0][0], stop=False, is_transpose=True)
-            for b, cols in here:
-                nc.tensor.matmul(total[:, cols], values[:, cols], identity[:], start=False, stop=b == last, is_transpose=True)
-            nc.scalar.activation(values, total[:, :width], COPY, scale=half_gain["page_bf"][:, t : t + 1])
-            nc.vector.tensor_tensor(values, values, weights_of(t, 1)[:, first : first + width], MULT)
-            nc.vector.tensor_copy(pages[t][:].indirect(columns(list3, N + first, width)), values)
+        t2[2] = held("t2_2", [P, PACK, P], F32)
+        t1[4] = held("t1_4", [P, PACK, P], F32)
+        for b in (2, 3):
+            open_second(b)
+            close_second(b)
+            second_slope(b)
+        for b in (4, 5):
+            first_slope(b)
+        late_step(2)
+        d1[2] = held("pair", [P, Q], U32)
+        quantise_step(2)
+        staged = held("woven3", [P, Q], F32)
+        values = held("values0_%d" % Q, [P, Q], F32)
+        make_values(values[:], 7, 0, Q, Q, staged[:])
+        put(values[:], 0, Q, Q)
+        for b in (6, 7):
+            first_slope(b)
+        woven[3] = held("woven3", [P, Q, PACK], BF16)
+        late_step(3)
+        quantise_step(3)
+        piece(6, 1, Q, Q)
+        piece(7, 2, Q, Q)
+        last = held("values_last", [P, S - Q], F32)
+        make_values(last[:, :Q], 6, 3, Q, Q)
+        for q in (2, 3):
+            for b in (2 * q, 2 * q + 1):
+                open_second(b)
+                close_second(b)
+                second_slope(b)
+            piece(7 - q % 2, 0, q * Q, Q)
+        piece(7, 1, N, N)
+        piece(6, 2, N, N)
+        make_values(last[:, Q:], 7, 3, N, N)
+        put(last[:], 3, Q, S - Q)
 
-        turned_piece(0, 5, 0, 0, Q)
-        turned_piece(0, 7, 4, Q, Q)
-        turned_piece(1, 2, 1)
-        turned_piece(2, 3, 6)
-        term[3, 0, 0] = late_terms[:, PACK, :]
-        open_second(0, 3, 0, 0, N)
-        second_slope(3, 0, 0, N)
-        put(3, 0, 0, N, "wgs01")
-        turned_piece(3, 5, 0)
+        page_bf = held("wgs%d" % N, [P, T2, PACK], BF16)
 
-        page_bf = held("page_bf", [P, T2, PACK], BF16)
-        rounded = held("wgs11", [P, 2, T2], BF16)
-        one = held("wgs10", [P, 1], F32)
-        nc.gpsimd.memset(one[:], 1.0)
+        def round_plane(copy, t, first, width):
+            copy(out=page_bf[:, first : first + width, t], in_=pages[t][:, first : first + width])
 
-        def pair_write(copy, first, width):
-            copy(out=page_bf[:, first : first + width, 2:], in_=rounded[:, :, first : first + width].rearrange("p e n -> p n e"))
-
+        low, mid, shared = 3 * P, 7 * P, 9 * P
         for t in range(2):
-            for c in range(chunks):
-                nc.scalar.copy(out=page_bf[:, c * N : (c + 1) * N, t], in_=pages[t][:, c * N : (c + 1) * N])
-        for c in range(2):
-            cols = slice(c * N, (c + 1) * N)
-            nc.gpsimd.tensor_scalar(page_bf[:, cols, 2:], pages[2][:, cols].unsqueeze(2).to_broadcast([P, N, 2]), one[:], 0.0, MULT, ADD)
-        nc.gpsimd.tensor_scalar(rounded[:, 0, 2 * N :], pages[2][:, 2 * N :], 1.0, 0.0, MULT, ADD)
+            round_plane(gpsimd_round, t, 0, shared)
+            round_plane(nc.scalar.copy, t, shared, T2 - shared)
+        flat = held("page1", [P, 2, mid - low], BF16)
+        round_plane(gpsimd_round, 2, 0, low)
+        gpsimd_round(flat[:, 0, :], pages[2][:, low:mid])
+        round_plane(nc.scalar.copy, 2, mid, T2 - mid)
 
-        page_q = [held("page_q%d" % c, [P, N], U32) for c in range(chunks)]
-        page_s = [held("page_s%d" % c, [P, N], U8) for c in range(chunks)]
+        v2_w = held("page0", [P, S2], U32)
+        nc.vector.tensor_copy(out=v2_w[:], in_=tab2_w[:].bitcast(U32).indirect(list2[:]))
 
-        def round_last(copy, first, width):
-            copy(out=rounded[:, 1, first : first + width], in_=pages[3][:, first : first + width])
+        page_q = held("page_q", [P, T2], U32)
+        page_s = held("page_s", [P, T2], U8)
 
         def quantise_page(first, width):
-            c, lo = divmod(first, N)
-            cols = slice(lo, lo + width)
-            nc.vector.quantize_mx(out=page_q[c][:, cols].bitcast(FP8X4), scales=page_s[c][:, cols], in_=page_bf[:, first : first + width, :].rearrange("p n t -> p (n t)"))
+            cols = slice(first, first + width)
+            nc.vector.quantize_mx(out=page_q[:, cols].bitcast(FP8X4), scales=page_s[:, cols], in_=page_bf[:, cols, :].rearrange("p n t -> p (n t)"))
 
-        round_last(nc.scalar.copy, 3 * N - P, N + P)
-        pair_write(nc.scalar.copy, 3 * N, N)
-        pair_write(nc.scalar.copy, 3 * N - P, P)
-        for c in range(2):
-            nc.vector.tensor_copy(out=page_bf[:, c * N : (c + 1) * N, 3], in_=pages[3][:, c * N : (c + 1) * N])
-        round_last(nc.vector.tensor_copy, 2 * N, N - P)
-        quantise_page(0, N)
-        pair_write(nc.vector.tensor_copy, 2 * N, N - P)
-        quantise_page(N, N)
-        quantise_page(2 * N, Q)
-        quantise_page(3 * N, N)
-        quantise_page(3 * N - P, P)
-        quantise_page(2 * N + Q, P)
+        round_plane(gpsimd_round, 3, 0, low)
+        round_plane(nc.scalar.copy, 3, 2 * N, N)
+        round_plane(nc.scalar.copy, 3, mid, 2 * N - mid)
+        round_plane(nc.scalar.copy, 3, 3 * N, Q)
+        round_plane(nc.scalar.copy, 3, 3 * N + Q, Q)
+        nc.vector.tensor_copy(out=flat[:, 1, :], in_=pages[3][:, low:mid])
+        nc.vector.tensor_copy(out=page_bf[:, low:mid, 2:], in_=flat[:].rearrange("p e n -> p n e"))
+        cuts = [(0, N), (2 * N, N), (N, N), (3 * N, Q), (3 * N + Q, Q)]
+        for first, width in cuts:
+            quantise_page(first, width)
 
         def score(b, scores, n, first, width, copy):
             acc = bank(b)
-            c, lo = divmod(first, N)
-            nc.tensor.matmul_mx(
-                out=acc[:, :width], lhsT=v2_w[:, n * P : (n + 1) * P].bitcast(FP8X4), lhsT_scale=v2_s[:, n * P : (n + 1) * P],
-                rhs=page_q[c][:, lo : lo + width].bitcast(FP8X4), rhs_scale=page_s[c][:, lo : lo + width], start=True, stop=True,
-            )
-            copy(out=scores[:, first : first + width], in_=acc[:, :width])
+            cols = slice(first, first + width)
+            mx(acc[:, :width], (v2_w[:, n * P : (n + 1) * P], v2_s[:, n * P : (n + 1) * P]), FP8X4, page_q[:, cols], page_s[:, cols], True, True)
+            copy(out=scores[:, cols], in_=acc[:, :width])
 
         for n in range(boats):
-            scores = held(("scores0", "scores1", "w_raw")[n % 3], [P, T2], F32)
+            scores = held("scores%d" % (n % 3), [P, T2], F32)
             if n == 0:
-                score(0, scores, n, 0, N, nc.scalar.copy)
-                score(1, scores, n, N, N, nc.scalar.copy)
-                score(4, scores, n, 2 * N, Q, nc.scalar.copy)
-                score(2, scores, n, 3 * N, N, nc.scalar.copy)
-                score(5, scores, n, 3 * N - P, P, nc.scalar.copy)
-                score(3, scores, n, 2 * N + Q, P, nc.vector.tensor_copy)
+                for i, (first, width) in enumerate(cuts):
+                    score(i, scores, n, first, width, nc.vector.tensor_copy if i == len(cuts) - 1 else nc.scalar.copy)
             else:
-                for b, c in ((0, 3), (2, 0), (3, 1), (1, 2)):
-                    score(b, scores, n, c * N, N, nc.scalar.copy)
+                for i, c in enumerate((0, 2, 1, 3)):
+                    score((5 + 4 * (n - 1) + i) % 8, scores, n, c * N, N, nc.scalar.copy)
             pieces = [(0, PICK)] if n < boats - 1 else [(0, N), (N, N - P), (PICK - P, P)]
             for first, width in pieces:
-                picked = held(("t1_0", "t1_1", "flat")[n] if n < boats - 1 else "picked%d" % first, [P, width], F32)
+                picked = held(("w_raw0", "w_raw1", "wgs0")[n] if n < 3 else "picked%d" % first, [P, width], F32)
                 nc.vector.tensor_tensor(picked[:], scores[:].indirect(columns(list4, first, width)), reach_sb[n][:, first : first + width], MULT)
                 nc.sync.dma_start(out=out[n * P : (n + 1) * P, first : first + width], in_=picked[:])

@@ -45,11 +45,8 @@ def tile_list_lifeboat_heun_scores_kernel(
             return psum.tile([P, N], F32, name="bank%d" % b)
 
         def load_scale_rows(plane, rows):
-            for q in range(4):
-                nc.sync.dma_start(
-                    out=plane[32 * q : 32 * q + 4, :].bitcast(I32),
-                    in_=rows[0, 4 * q : 4 * q + 4, :].bitcast(I32),
-                )
+            for r in range(4):
+                nc.sync.dma_start(out=plane[r:P:32, :].bitcast(I32), in_=rows[0, r:16:4, :].bitcast(I32))
 
         def words_of(table):
             return table[0].rearrange("p n i -> p (n i)").bitcast(I32)
@@ -186,8 +183,8 @@ def tile_list_lifeboat_heun_scores_kernel(
         def by_plane(acc):
             return acc[:].rearrange("p (t m) -> p t m", t=PACK)
 
-        def first_slope(b):
-            z1 = bank(b % 2)
+        def first_slope(b, z_bank=None):
+            z1 = bank(b % 2 if z_bank is None else z_bank)
             forcing_pass(z1, b)
             drift_pass(z1, entries(b), True)
             nc.scalar.activation(t1[b][:], by_plane(z1), TANH)
@@ -207,7 +204,7 @@ def tile_list_lifeboat_heun_scores_kernel(
             nc.vector.quantize_mx(out=d1[q][:, cols].bitcast(FP8X4), scales=d1_s[q][:, cols], in_=woven[q][:, cols, :].rearrange("p n t -> p (n t)"))
 
         def open_second(b):
-            z2[b] = bank(4 + b % 2)
+            z2[b] = bank(4 + b % 2 if b < 6 else b % 2)
             forcing_pass(z2[b], b)
             drift_pass(z2[b], entries(b), False)
 
@@ -272,6 +269,9 @@ def tile_list_lifeboat_heun_scores_kernel(
             )
         for b in range(2):
             quantise_step(0, b * P, P)
+        first_slope(2, 7)
+        first_step(2)
+        first_slope(3, 0)
 
         def upright_second(z_bank, planes):
             z = bank(z_bank)
@@ -287,8 +287,10 @@ def tile_list_lifeboat_heun_scores_kernel(
 
         for t in range(2):
             upright_second(4 + t, [t])
+        first_step(3)
         both = held("pair", [P, 2, Q], F32)
         nc.vector.tensor_tensor(both[:], up2[:, :2, :], up1[:, :2, :], ADD)
+        quantise_step(1)
         values = [held("values%d_0" % t, [P, Q], F32) for t in range(2)]
         for t in range(2):
             nc.vector.scalar_tensor_tensor(values[t][:], both[:, t, :], half_gain[:, t : t + 1], weights_of(t, 0, Q), MULT, MULT)
@@ -300,10 +302,6 @@ def tile_list_lifeboat_heun_scores_kernel(
         pair = held("pair", [P, 2, Q], F32)
         nc.gpsimd.tensor_tensor(pair[:], up2[:, rows, :], up1[:, rows, :], ADD)
         nc.gpsimd.tensor_tensor(pair[:], pair[:], wgs_sb[0][:, rows, :], MULT)
-        for b in (2, 3):
-            first_slope(b)
-            first_step(b)
-        quantise_step(1)
         for t in (2, 3):
             put(pair[:, t - 2, :], t, 0, Q)
 
@@ -329,20 +327,20 @@ def tile_list_lifeboat_heun_scores_kernel(
             close_second(b)
             second_slope(b)
         for b in (4, 5):
-            first_slope(b)
+            first_slope(b, 1 - b % 2)
         late_step(2)
         d1[2] = held("pair", [P, Q], U32)
         quantise_step(2)
+        piece(7, 0, Q, Q)
         staged = held("woven3", [P, Q], F32)
-        values = held("values0_%d" % Q, [P, Q], F32)
-        make_values(values[:], 7, 0, Q, Q, staged[:])
-        put(values[:], 0, Q, Q)
+        values = held("values1_%d" % Q, [P, Q], F32)
+        make_values(values[:], 6, 1, Q, Q, staged[:])
+        put(values[:], 1, Q, Q)
         for b in (6, 7):
-            first_slope(b)
+            first_slope(b, 1 - b % 2)
         woven[3] = held("woven3", [P, Q, PACK], BF16)
         late_step(3)
         quantise_step(3)
-        piece(6, 1, Q, Q)
         piece(7, 2, Q, Q)
         last = held("values_last", [P, S - Q], F32)
         make_values(last[:, :Q], 6, 3, Q, Q)
@@ -351,25 +349,30 @@ def tile_list_lifeboat_heun_scores_kernel(
                 open_second(b)
                 close_second(b)
                 second_slope(b)
-            piece(7 - q % 2, 0, q * Q, Q)
-        piece(7, 1, N, N)
-        piece(6, 2, N, N)
-        make_values(last[:, Q:], 7, 3, N, N)
+            for t in range(2):
+                piece(7 - t if q == 2 else 2 * t + 5, t, q * Q, Q)
+        piece(3, 2, N, N)
+        make_values(last[:, Q:], 4, 3, N, N)
         put(last[:], 3, Q, S - Q)
 
-        page_bf = held("wgs%d" % N, [P, T2, PACK], BF16)
+        side = T2 // 2
+        page_bf = [held(name, [P, side, PACK], BF16) for name in ("wgs%d" % N, "half_gain")]
+
+        def woven_page(first, width):
+            return page_bf[first // side][:, first % side : first % side + width, :]
 
         def round_plane(copy, t, first, width):
-            copy(out=page_bf[:, first : first + width, t], in_=pages[t][:, first : first + width])
+            copy(out=woven_page(first, width)[:, :, t], in_=pages[t][:, first : first + width])
 
-        low, mid, shared = 3 * P, 7 * P, 9 * P
+        low, mid = 3 * P, 7 * P
         for t in range(2):
-            round_plane(gpsimd_round, t, 0, shared)
-            round_plane(nc.scalar.copy, t, shared, T2 - shared)
+            round_plane(gpsimd_round, t, 0, side)
+            round_plane(nc.scalar.copy, t, side, side)
         flat = held("page1", [P, 2, mid - low], BF16)
         round_plane(gpsimd_round, 2, 0, low)
         gpsimd_round(flat[:, 0, :], pages[2][:, low:mid])
-        round_plane(nc.scalar.copy, 2, mid, T2 - mid)
+        round_plane(nc.scalar.copy, 2, side, side)
+        round_plane(nc.scalar.copy, 2, mid, side - mid)
 
         v2_w = held("page0", [P, S2], U32)
         nc.vector.tensor_copy(out=v2_w[:], in_=tab2_w[:].bitcast(U32).indirect(list2[:]))
@@ -379,7 +382,7 @@ def tile_list_lifeboat_heun_scores_kernel(
 
         def quantise_page(first, width):
             cols = slice(first, first + width)
-            nc.vector.quantize_mx(out=page_q[:, cols].bitcast(FP8X4), scales=page_s[:, cols], in_=page_bf[:, cols, :].rearrange("p n t -> p (n t)"))
+            nc.vector.quantize_mx(out=page_q[:, cols].bitcast(FP8X4), scales=page_s[:, cols], in_=woven_page(first, width).rearrange("p n t -> p (n t)"))
 
         round_plane(gpsimd_round, 3, 0, low)
         round_plane(nc.scalar.copy, 3, 2 * N, N)
@@ -387,7 +390,7 @@ def tile_list_lifeboat_heun_scores_kernel(
         round_plane(nc.scalar.copy, 3, 3 * N, Q)
         round_plane(nc.scalar.copy, 3, 3 * N + Q, Q)
         nc.vector.tensor_copy(out=flat[:, 1, :], in_=pages[3][:, low:mid])
-        nc.vector.tensor_copy(out=page_bf[:, low:mid, 2:], in_=flat[:].rearrange("p e n -> p n e"))
+        nc.vector.tensor_copy(out=woven_page(low, mid - low)[:, :, 2:], in_=flat[:].rearrange("p e n -> p n e"))
         cuts = [(0, N), (2 * N, N), (N, N), (3 * N, Q), (3 * N + Q, Q)]
         for first, width in cuts:
             quantise_page(first, width)

@@ -48,6 +48,13 @@ def tile_list_lifeboat_heun_scores_kernel(
             for r in range(4):
                 nc.sync.dma_start(out=plane[r:P:32, :].bitcast(I32), in_=rows[0, r:16:4, :].bitcast(I32))
 
+        def load_spread(plane, rows):
+            nc.sync.dma_start(out=plane[0:P:8, :].bitcast(I32), in_=rows[0].bitcast(I32))
+
+        def move_scale_rows(plane, spread):
+            for r in range(4):
+                nc.sync.dma_start(out=plane[r:P:32, :].bitcast(I32), in_=spread[8 * r : P : 32, :].bitcast(I32))
+
         def words_of(table):
             return table[0].rearrange("p n i -> p (n i)").bitcast(I32)
 
@@ -73,8 +80,13 @@ def tile_list_lifeboat_heun_scores_kernel(
 
         nc.gpsimd.memset(tab_s[:, : T // 2].bitcast(I32), 0)
         nc.vector.memset(tab_s[:, T // 2 :].bitcast(I32), 0)
-        nc.vector.memset(wf_s_raw[:].bitcast(I32), 0)
         nc.vector.memset(tab2_s[:].bitcast(I32), 0)
+        nc.vector.memset(wf_s_raw[:].bitcast(I32), 0)
+
+        v_s = held("v_s", [P, S], U8)
+        v2_s = held("v2_s", [P, S2], U8)
+        nc.vector.memset(v_s[:].bitcast(I32), 0)
+        nc.vector.memset(v2_s[:].bitcast(I32), 0)
 
         identity = held("identity", [P, P], F32)
         make_identity(nc, identity[:])
@@ -88,15 +100,21 @@ def tile_list_lifeboat_heun_scores_kernel(
                 nc.sync.dma_start(out=wgs_sb[first][32 * q : 32 * q + 32], in_=wgs_rows[:, :, first : first + width])
 
         nc.sync.dma_start(list1[:], offs)
-        nc.sync.dma_start(out=gain_sb[:], in_=gain.rearrange("(p t) -> p t", t=PACK))
+        nc.sync.dma_start(out=tab_w[:, : T // 4], in_=words_of(tab_words)[:, : T // 4])
         nc.sync.dma_start(out=wf_raw[:].bitcast(I32), in_=wf_words[0].bitcast(I32))
-        load_scale_rows(tab_s, tab_scales)
-        nc.sync.dma_start(out=tab_w[:], in_=words_of(tab_words))
+        load_spread(tab_s, tab_scales)
+        nc.sync.dma_start(list2[:], offs2)
+        load_spread(tab2_s, tab2_scales)
+        nc.sync.dma_start(out=tab_w[:, T // 4 :], in_=words_of(tab_words)[:, T // 4 :])
         load_scale_rows(wf_s_raw, wf_scales)
         for u in range(2):
             nc.sync.dma_start(out=w_raw[u][:], in_=w_rows[:, :, u * Q : (u + 1) * Q])
-        nc.sync.dma_start(list2[:], offs2)
-        load_scale_rows(tab2_s, tab2_scales)
+        v_spread = held("v_spread", [P, S], U8)
+        v2_spread = held("v2_spread", [P, S2], U8)
+        nc.vector.tensor_copy(out=v_spread[:], in_=tab_s[:].indirect(list1[:]))
+        nc.vector.tensor_copy(out=v2_spread[:], in_=tab2_s[:].indirect(list2[:]))
+        move_scale_rows(v_s, v_spread)
+        nc.sync.dma_start(out=gain_sb[:], in_=gain.rearrange("(p t) -> p t", t=PACK))
         load_wgs(*wgs_cuts[0])
         nc.sync.dma_start(list3[:], offs3)
         for t in range(PACK):
@@ -104,20 +122,18 @@ def tile_list_lifeboat_heun_scores_kernel(
         load_wgs(*wgs_cuts[1])
         load_wgs(*wgs_cuts[2])
         nc.sync.dma_start(out=tab2_w[:], in_=words_of(tab2_words))
+        move_scale_rows(v2_s, v2_spread)
         nc.sync.dma_start(list4[:], offs4)
         for n in range(boats):
             nc.sync.dma_start(out=reach_sb[n][:], in_=reach[n * P : (n + 1) * P, :])
 
         v_w = [held("v_w%d" % h, [P, N], U32) for h in range(halves)]
-        v_s = [held("v_s%d" % h, [P, N], U8) for h in range(halves)]
         wf = held("wf", [P, 2 * H], U8)
         wf_s = held("wf_s", [P, H], U8)
         nc.vector.tensor_copy(
             out=wf[:].bitcast(U16).rearrange("p (t m) -> p t m", t=PACK),
             in_=wf_raw[:].bitcast(U16).rearrange("p (m t) -> p t m", t=PACK),
         )
-        for h in range(halves):
-            nc.vector.tensor_copy(out=v_s[h][:], in_=tab_s[:].indirect(columns(list1, h * N, N)))
         for h in range(halves):
             nc.vector.tensor_copy(out=v_w[h][:], in_=tab_w[:].bitcast(U32).indirect(columns(list1, h * N, N)))
         nc.gpsimd.tensor_copy(
@@ -152,12 +168,10 @@ def tile_list_lifeboat_heun_scores_kernel(
         for t, name in ((2, "t2_2"), (3, "t1_4")):
             early_gain[t] = held(name, [P, 1], F32)
             nc.gpsimd.tensor_scalar(early_gain[t][:], gain_sb[:, t : t + 1], 0.5, 0.0, MULT, ADD)
-        v2_s = held("v2_s", [P, S2], U8)
-        nc.vector.tensor_copy(out=v2_s[:], in_=tab2_s[:].indirect(list2[:]))
 
         def entries(b):
             h, lo = divmod(b * P, N)
-            return v_w[h][:, lo : lo + P], v_s[h][:, lo : lo + P]
+            return v_w[h][:, lo : lo + P], v_s[:, b * P : (b + 1) * P]
 
         def mx(acc, left, fmt, codes, scales, start, stop):
             nc.tensor.matmul_mx(
@@ -278,7 +292,7 @@ def tile_list_lifeboat_heun_scores_kernel(
             for e, t in enumerate(planes):
                 for b in range(2):
                     upright(z[:, e * Q + b * P : e * Q + (b + 1) * P], t, FP4X4, *entries(b), e == 0 and b == 0, False)
-                upright(z[:, e * Q : (e + 1) * Q], t, FP8X4, v_w[0][:, :Q], v_s[0][:, :Q], False, False)
+                upright(z[:, e * Q : (e + 1) * Q], t, FP8X4, v_w[0][:, :Q], v_s[:, :Q], False, False)
             for e, t in enumerate(planes):
                 upright(z[:, e * Q : (e + 1) * Q], t, FP8X4, d1[0][:], d1_s[0][:], False, t == planes[-1])
             rows = slice(planes[0], planes[-1] + 1)
@@ -364,7 +378,7 @@ def tile_list_lifeboat_heun_scores_kernel(
         def round_plane(copy, t, first, width):
             copy(out=woven_page(first, width)[:, :, t], in_=pages[t][:, first : first + width])
 
-        low, mid = 3 * P, 7 * P
+        low, mid = 4 * P, 7 * P
         for t in range(2):
             round_plane(gpsimd_round, t, 0, side)
             round_plane(nc.scalar.copy, t, side, side)

@@ -31,7 +31,6 @@ def tile_list_lifeboat_heun_scores_kernel(
     w, wf_words, wf_scales, gain, page0, wgs, reach, out,
 ):
     nc = tc.nc
-    halves = S // N
     boats = S2 // P
 
     with ExitStack() as ctx:
@@ -127,15 +126,14 @@ def tile_list_lifeboat_heun_scores_kernel(
         for n in range(boats):
             nc.sync.dma_start(out=reach_sb[n][:], in_=reach[n * P : (n + 1) * P, :])
 
-        v_w = [held("v_w%d" % h, [P, N], U32) for h in range(halves)]
+        v_w = {0: held("v_w0", [P, N], U32)}
         wf = held("wf", [P, 2 * H], U8)
         wf_s = held("wf_s", [P, H], U8)
         nc.vector.tensor_copy(
             out=wf[:].bitcast(U16).rearrange("p (t m) -> p t m", t=PACK),
             in_=wf_raw[:].bitcast(U16).rearrange("p (m t) -> p t m", t=PACK),
         )
-        for h in range(halves):
-            nc.vector.tensor_copy(out=v_w[h][:], in_=tab_w[:].bitcast(U32).indirect(columns(list1, h * N, N)))
+        nc.vector.tensor_copy(out=v_w[0][:], in_=tab_w[:].bitcast(U32).indirect(columns(list1, 0, N)))
         nc.gpsimd.tensor_copy(
             out=wf_s[:].rearrange("p (t m) -> p t m", t=PACK),
             in_=wf_s_raw[:].rearrange("p (m t) -> p t m", t=PACK),
@@ -156,18 +154,15 @@ def tile_list_lifeboat_heun_scores_kernel(
             cols = slice(u * Q, (u + 1) * Q)
             nc.vector.quantize_mx(out=wq[:, cols].bitcast(FP8X4), scales=wq_s[:, cols], in_=w_bf[u][:].rearrange("p t m j -> p (t m j)"))
 
-        for u in range(2):
-            round_w(nc.scalar.copy, 0, u)
-        round_w(nc.vector.tensor_copy, 1, 0)
-        round_w(nc.scalar.copy, 1, 1)
+        for part in range(2):
+            round_w(nc.vector.tensor_copy, part, 0)
+            round_w(nc.scalar.copy, part, 1)
         for u in range(2):
             quantise_w(u)
+        v_w[1] = held("w_bf1", [P, N], U32)
+        nc.vector.tensor_copy(out=v_w[1][:], in_=tab_w[:].bitcast(U32).indirect(columns(list1, N, N)))
         half_gain = held("half_gain", [P, PACK], F32)
         nc.gpsimd.tensor_scalar(half_gain[:], gain_sb[:], 0.5, 0.0, MULT, ADD)
-        early_gain = {}
-        for t, name in ((2, "t2_2"), (3, "t1_4")):
-            early_gain[t] = held(name, [P, 1], F32)
-            nc.gpsimd.tensor_scalar(early_gain[t][:], gain_sb[:, t : t + 1], 0.5, 0.0, MULT, ADD)
 
         def entries(b):
             h, lo = divmod(b * P, N)
@@ -187,8 +182,8 @@ def tile_list_lifeboat_heun_scores_kernel(
             mx(acc[:, cols], left, FP8X4, wq[:, cols], wq_s[:, cols], False, stop)
 
         blocks = S // P
-        t1 = {b: held("t1_%d" % b, [P, PACK, P], F32) for b in range(2, blocks) if b != 4}
-        t2 = {b: held("t2_%d" % b, [P, PACK, P], F32) for b in range(3, blocks)}
+        t1 = {b: held("t1_%d" % b, [P, PACK, P], F32) for b in range(2, blocks)}
+        t2 = {b: held("t2_%d" % b, [P, PACK, P], F32) for b in range(2, blocks)}
         woven = {q: held("woven%d" % q, [P, Q, PACK], BF16) for q in range(3)}
         d1 = {q: held("d1_%d" % q, [P, Q], U32) for q in (0, 1, 3)}
         d1_s = [held("d1_s%d" % q, [P, Q], U8) for q in range(S // Q)]
@@ -311,7 +306,7 @@ def tile_list_lifeboat_heun_scores_kernel(
         for t in range(2):
             put(values[t][:], t, 0, Q)
         for t in (2, 3):
-            nc.scalar.activation(weights_of(t, 0, Q), weights_of(t, 0, Q), COPY, scale=early_gain[t][:])
+            nc.gpsimd.tensor_scalar(weights_of(t, 0, Q), weights_of(t, 0, Q), half_gain[:, t : t + 1], 0.0, MULT, ADD)
         rows = upright_second(6, [2, 3])
         pair = held("pair", [P, 2, Q], F32)
         nc.gpsimd.tensor_tensor(pair[:], up2[:, rows, :], up1[:, rows, :], ADD)
@@ -334,8 +329,6 @@ def tile_list_lifeboat_heun_scores_kernel(
                     nc.scalar.activation(flat[:, t, :], back[:, e * Q : (e + 1) * Q], COPY, scale=gain_sb[:, t : t + 1])
             gpsimd_round(woven[q][:], flat[:].rearrange("p t n -> p n t"))
 
-        t2[2] = held("t2_2", [P, PACK, P], F32)
-        t1[4] = held("t1_4", [P, PACK, P], F32)
         for b in (2, 3):
             open_second(b)
             close_second(b)
@@ -346,12 +339,12 @@ def tile_list_lifeboat_heun_scores_kernel(
         d1[2] = held("pair", [P, Q], U32)
         quantise_step(2)
         piece(7, 0, Q, Q)
+        for b in (6, 7):
+            first_slope(b, 1 - b % 2)
         staged = held("woven3", [P, Q], F32)
         values = held("values1_%d" % Q, [P, Q], F32)
         make_values(values[:], 6, 1, Q, Q, staged[:])
         put(values[:], 1, Q, Q)
-        for b in (6, 7):
-            first_slope(b, 1 - b % 2)
         woven[3] = held("woven3", [P, Q, PACK], BF16)
         late_step(3)
         quantise_step(3)
@@ -364,9 +357,9 @@ def tile_list_lifeboat_heun_scores_kernel(
                 close_second(b)
                 second_slope(b)
             for t in range(2):
-                piece(7 - t if q == 2 else 2 * t + 5, t, q * Q, Q)
-        piece(3, 2, N, N)
-        make_values(last[:, Q:], 4, 3, N, N)
+                piece(7 - t if q == 2 else 2 + t, t, q * Q, Q)
+        piece(4, 2, N, N)
+        make_values(last[:, Q:], 5, 3, N, N)
         put(last[:], 3, Q, S - Q)
 
         side = T2 // 2
@@ -378,15 +371,14 @@ def tile_list_lifeboat_heun_scores_kernel(
         def round_plane(copy, t, first, width):
             copy(out=woven_page(first, width)[:, :, t], in_=pages[t][:, first : first + width])
 
-        low, mid = 4 * P, 7 * P
+        low = 3 * P
         for t in range(2):
             round_plane(gpsimd_round, t, 0, side)
             round_plane(nc.scalar.copy, t, side, side)
-        flat = held("page1", [P, 2, mid - low], BF16)
+        flat = held("page1", [P, 2, side - low], BF16)
         round_plane(gpsimd_round, 2, 0, low)
-        gpsimd_round(flat[:, 0, :], pages[2][:, low:mid])
+        gpsimd_round(flat[:, 0, :], pages[2][:, low:side])
         round_plane(nc.scalar.copy, 2, side, side)
-        round_plane(nc.scalar.copy, 2, mid, side - mid)
 
         v2_w = held("page0", [P, S2], U32)
         nc.vector.tensor_copy(out=v2_w[:], in_=tab2_w[:].bitcast(U32).indirect(list2[:]))
@@ -400,29 +392,36 @@ def tile_list_lifeboat_heun_scores_kernel(
 
         round_plane(gpsimd_round, 3, 0, low)
         round_plane(nc.scalar.copy, 3, 2 * N, N)
-        round_plane(nc.scalar.copy, 3, mid, 2 * N - mid)
         round_plane(nc.scalar.copy, 3, 3 * N, Q)
-        round_plane(nc.scalar.copy, 3, 3 * N + Q, Q)
-        nc.vector.tensor_copy(out=flat[:, 1, :], in_=pages[3][:, low:mid])
-        nc.vector.tensor_copy(out=woven_page(low, mid - low)[:, :, 2:], in_=flat[:].rearrange("p e n -> p n e"))
-        cuts = [(0, N), (2 * N, N), (N, N), (3 * N, Q), (3 * N + Q, Q)]
+        round_plane(nc.scalar.copy, 3, 3 * N + Q, P)
+        round_plane(nc.scalar.copy, 3, T2 - P, P)
+        nc.vector.tensor_copy(out=flat[:, 1, :], in_=pages[3][:, low:side])
+        nc.vector.tensor_copy(out=woven_page(low, side - low)[:, :, 2:], in_=flat[:].rearrange("p e n -> p n e"))
+        cuts = [(2 * N, N), (0, N), (N, N), (3 * N, Q), (3 * N + Q, P), (T2 - P, P)]
         for first, width in cuts:
             quantise_page(first, width)
 
-        def score(b, scores, n, first, width, copy):
+        def score(b, scores, n, parts, copy):
             acc = bank(b)
-            cols = slice(first, first + width)
-            mx(acc[:, :width], (v2_w[:, n * P : (n + 1) * P], v2_s[:, n * P : (n + 1) * P]), FP8X4, page_q[:, cols], page_s[:, cols], True, True)
-            copy(out=scores[:, cols], in_=acc[:, :width])
+            base = parts[0][0]
+            for first, width in parts:
+                cols = slice(first, first + width)
+                mx(
+                    acc[:, first - base : first - base + width], (v2_w[:, n * P : (n + 1) * P], v2_s[:, n * P : (n + 1) * P]),
+                    FP8X4, page_q[:, cols], page_s[:, cols], True, True,
+                )
+            total = sum(width for first, width in parts)
+            copy(out=scores[:, base : base + total], in_=acc[:, :total])
 
         for n in range(boats):
             scores = held("scores%d" % (n % 3), [P, T2], F32)
             if n == 0:
-                for i, (first, width) in enumerate(cuts):
-                    score(i, scores, n, first, width, nc.vector.tensor_copy if i == len(cuts) - 1 else nc.scalar.copy)
+                for i in range(4):
+                    score(i, scores, n, cuts[i : i + 1], nc.scalar.copy)
+                score(4, scores, n, cuts[4:], nc.vector.tensor_copy)
             else:
-                for i, c in enumerate((0, 2, 1, 3)):
-                    score((5 + 4 * (n - 1) + i) % 8, scores, n, c * N, N, nc.scalar.copy)
+                for i, c in enumerate((2, 0, 1, 3)):
+                    score((5 + 4 * (n - 1) + i) % 8, scores, n, [(c * N, N)], nc.scalar.copy)
             pieces = [(0, PICK)] if n < boats - 1 else [(0, N), (N, N - P), (PICK - P, P)]
             for first, width in pieces:
                 picked = held(("w_raw0", "w_raw1", "wgs0")[n] if n < 3 else "picked%d" % first, [P, width], F32)

@@ -94,9 +94,13 @@ def tile_list_lifeboat_heun_scores_kernel(
         wgs_rows = wgs.rearrange("(m t) j -> m t j", t=PACK)
         w_rows = w.rearrange("(p j) c -> p j c", j=PACK)
 
-        def load_wgs(first, width):
+        def load_wgs(first):
+            base = min(first, N)
             for q in (0, 2, 1, 3):
-                nc.sync.dma_start(out=wgs_sb[first][32 * q : 32 * q + 32], in_=wgs_rows[:, :, first : first + width])
+                nc.sync.dma_start(
+                    out=wgs_sb[base][32 * q : 32 * q + 32, :, first - base : first - base + Q],
+                    in_=wgs_rows[:, :, first : first + Q],
+                )
 
         nc.sync.dma_start(list1[:], offs)
         nc.sync.dma_start(out=tab_w[:, : T // 4], in_=words_of(tab_words)[:, : T // 4])
@@ -114,13 +118,14 @@ def tile_list_lifeboat_heun_scores_kernel(
         nc.vector.tensor_copy(out=v2_spread[:], in_=tab2_s[:].indirect(list2[:]))
         move_scale_rows(v_s, v_spread)
         nc.sync.dma_start(out=gain_sb[:], in_=gain.rearrange("(p t) -> p t", t=PACK))
-        load_wgs(*wgs_cuts[0])
+        load_wgs(0)
         nc.sync.dma_start(list3[:], offs3)
         for t in range(PACK):
             nc.sync.dma_start(out=pages[t][:], in_=page_rows[t])
-        load_wgs(*wgs_cuts[1])
-        load_wgs(*wgs_cuts[2])
+        load_wgs(Q)
         nc.sync.dma_start(out=tab2_w[:], in_=words_of(tab2_words))
+        load_wgs(2 * Q)
+        load_wgs(3 * Q)
         move_scale_rows(v2_s, v2_spread)
         nc.sync.dma_start(list4[:], offs4)
         for n in range(boats):
@@ -345,6 +350,8 @@ def tile_list_lifeboat_heun_scores_kernel(
         values = held("values1_%d" % Q, [P, Q], F32)
         make_values(values[:], 6, 1, Q, Q, staged[:])
         put(values[:], 1, Q, Q)
+        v2_w = held("v2_w", [P, S2], U32)
+        nc.vector.tensor_copy(out=v2_w[:], in_=tab2_w[:].bitcast(U32).indirect(list2[:]))
         woven[3] = held("woven3", [P, Q, PACK], BF16)
         late_step(3)
         quantise_step(3)
@@ -380,8 +387,6 @@ def tile_list_lifeboat_heun_scores_kernel(
         gpsimd_round(flat[:, 0, :], pages[2][:, low:side])
         round_plane(nc.scalar.copy, 2, side, side)
 
-        v2_w = held("page0", [P, S2], U32)
-        nc.vector.tensor_copy(out=v2_w[:], in_=tab2_w[:].bitcast(U32).indirect(list2[:]))
 
         page_q = held("page_q", [P, T2], U32)
         page_s = held("page_s", [P, T2], U8)

@@ -118,9 +118,10 @@ def tile_list_lifeboat_heun_scores_kernel(
         nc.vector.tensor_copy(out=v2_spread[:], in_=tab2_s[:].indirect(list2[:]))
         move_scale_rows(v_s, v_spread)
         nc.sync.dma_start(out=gain_sb[:], in_=gain.rearrange("(p t) -> p t", t=PACK))
+        nc.sync.dma_start(out=pages[0][:], in_=page_rows[0])
         load_wgs(0)
         nc.sync.dma_start(list3[:], offs3)
-        for t in range(PACK):
+        for t in range(1, PACK):
             nc.sync.dma_start(out=pages[t][:], in_=page_rows[t])
         load_wgs(Q)
         nc.sync.dma_start(out=tab2_w[:], in_=words_of(tab2_words))

@@ -121,12 +121,13 @@ def tile_list_lifeboat_heun_scores_kernel(
         nc.sync.dma_start(out=pages[0][:], in_=page_rows[0])
         load_wgs(0)
         nc.sync.dma_start(list3[:], offs3)
-        for t in range(1, PACK):
+        for t in range(1, PACK - 1):
             nc.sync.dma_start(out=pages[t][:], in_=page_rows[t])
         load_wgs(Q)
-        nc.sync.dma_start(out=tab2_w[:], in_=words_of(tab2_words))
         load_wgs(2 * Q)
         load_wgs(3 * Q)
+        nc.sync.dma_start(out=pages[PACK - 1][:], in_=page_rows[PACK - 1])
+        nc.sync.dma_start(out=tab2_w[:], in_=words_of(tab2_words))
         move_scale_rows(v2_s, v2_spread)
         nc.sync.dma_start(list4[:], offs4)
         for n in range(boats):
@@ -219,7 +220,7 @@ def tile_list_lifeboat_heun_scores_kernel(
             nc.vector.quantize_mx(out=d1[q][:, cols].bitcast(FP8X4), scales=d1_s[q][:, cols], in_=woven[q][:, cols, :].rearrange("p n t -> p (n t)"))
 
         def open_second(b):
-            z2[b] = bank(4 + b % 2 if b < 6 else b % 2)
+            z2[b] = bank(4 + b % 2 if b < 6 else (6, 2)[b % 2])
             forcing_pass(z2[b], b)
             drift_pass(z2[b], entries(b), False)
 
@@ -313,12 +314,16 @@ def tile_list_lifeboat_heun_scores_kernel(
             put(values[t][:], t, 0, Q)
         for t in (2, 3):
             nc.gpsimd.tensor_scalar(weights_of(t, 0, Q), weights_of(t, 0, Q), half_gain[:, t : t + 1], 0.0, MULT, ADD)
+        for b in (4, 5):
+            first_slope(b, 1 - b % 2)
         rows = upright_second(6, [2, 3])
         pair = held("pair", [P, 2, Q], F32)
         nc.gpsimd.tensor_tensor(pair[:], up2[:, rows, :], up1[:, rows, :], ADD)
-        nc.gpsimd.tensor_tensor(pair[:], pair[:], wgs_sb[0][:, rows, :], MULT)
-        for t in (2, 3):
-            put(pair[:, t - 2, :], t, 0, Q)
+        third = held("values2_0", [P, Q], F32)
+        last = held("values_last", [P, S], F32)
+        nc.gpsimd.tensor_tensor(third[:], pair[:, 0, :], weights_of(2, 0, Q), MULT)
+        nc.gpsimd.tensor_tensor(last[:, :Q], pair[:, 1, :], weights_of(3, 0, Q), MULT)
+        put(third[:], 2, 0, Q)
 
         def gpsimd_round(out, in_):
             nc.gpsimd.tensor_scalar(out, in_, 1.0, 0.0, MULT, ADD)
@@ -339,55 +344,74 @@ def tile_list_lifeboat_heun_scores_kernel(
             open_second(b)
             close_second(b)
             second_slope(b)
-        for b in (4, 5):
-            first_slope(b, 1 - b % 2)
         late_step(2)
-        d1[2] = held("pair", [P, Q], U32)
+        d1[2] = held("values2_0", [P, Q], U32)
         quantise_step(2)
         piece(7, 0, Q, Q)
         for b in (6, 7):
             first_slope(b, 1 - b % 2)
+        piece(6, 1, Q, Q)
         staged = held("woven3", [P, Q], F32)
-        values = held("values1_%d" % Q, [P, Q], F32)
-        make_values(values[:], 6, 1, Q, Q, staged[:])
-        put(values[:], 1, Q, Q)
-        v2_w = held("v2_w", [P, S2], U32)
-        nc.vector.tensor_copy(out=v2_w[:], in_=tab2_w[:].bitcast(U32).indirect(list2[:]))
+        values = held("values2_%d" % Q, [P, Q], F32)
+        make_values(values[:], 7, 2, Q, Q, staged[:])
+        put(values[:], 2, Q, Q)
         woven[3] = held("woven3", [P, Q, PACK], BF16)
         late_step(3)
         quantise_step(3)
-        piece(7, 2, Q, Q)
-        last = held("values_last", [P, S - Q], F32)
-        make_values(last[:, :Q], 6, 3, Q, Q)
+        make_values(last[:, Q:N], 6, 3, Q, Q)
         for q in (2, 3):
             for b in (2 * q, 2 * q + 1):
                 open_second(b)
                 close_second(b)
                 second_slope(b)
-            for t in range(2):
-                piece(7 - t if q == 2 else 2 + t, t, q * Q, Q)
-        piece(4, 2, N, N)
-        make_values(last[:, Q:], 5, 3, N, N)
-        put(last[:], 3, Q, S - Q)
+            for t in range(3):
+                piece((7, 6, 2)[t] if q == 2 else (3, 4, 5)[t], t, q * Q, Q)
+        staged = held("v2_w", [P, N], F32)
+        make_values(last[:, N:], 7, 3, N, N, staged[:])
+        put(last[:], 3, 0, S)
 
-        side = T2 // 2
-        page_bf = [held(name, [P, side, PACK], BF16) for name in ("wgs%d" % N, "half_gain")]
+        low = 3 * P
+        side = 2 * low
+        page_bf = held("tab_w", [P, T2, PACK], BF16)
+        left = held("wgs%d" % N, [P, 3, side], BF16)
+        right = held("half_gain", [P, 3, T2 - side], BF16)
 
         def woven_page(first, width):
-            return page_bf[first // side][:, first % side : first % side + width, :]
+            return page_bf[:, first : first + width, :]
 
         def round_plane(copy, t, first, width):
             copy(out=woven_page(first, width)[:, :, t], in_=pages[t][:, first : first + width])
 
-        low = 3 * P
-        for t in range(2):
-            round_plane(gpsimd_round, t, 0, side)
-            round_plane(nc.scalar.copy, t, side, side)
-        flat = held("page1", [P, 2, side - low], BF16)
-        round_plane(gpsimd_round, 2, 0, low)
-        gpsimd_round(flat[:, 0, :], pages[2][:, low:side])
-        round_plane(nc.scalar.copy, 2, side, side)
+        def round_left(copy, t, row, first, width):
+            copy(out=left[:, row, first : first + width], in_=pages[t][:, first : first + width])
 
+        def round_right(t, first, width):
+            nc.scalar.copy(out=right[:, t, first - side : first - side + width], in_=pages[t][:, first : first + width])
+
+        def weave_left(copy, planes, rows, first, width):
+            copy(out=woven_page(first, width)[:, :, planes], in_=left[:, rows, first : first + width].rearrange("p t n -> p n t"))
+
+        def weave_right(first, width):
+            nc.scalar.copy(
+                out=woven_page(first, width)[:, :, :3].rearrange("p (c i) t -> p c t i", i=2),
+                in_=right[:, :, first - side : first - side + width].rearrange("p t (c i) -> p c t i", i=2),
+            )
+
+        halves = [(side, (T2 - side) // 2), ((T2 + side) // 2, (T2 - side) // 2)]
+        for t in range(2):
+            round_right(t, side, T2 - side)
+        for first, width in halves:
+            round_right(2, first, width)
+        for t in range(2):
+            round_left(gpsimd_round, t, t, 0, side)
+        weave_left(gpsimd_round, slice(0, 2), slice(0, 2), low, low)
+        round_left(gpsimd_round, 2, 0, low, low)
+        round_left(gpsimd_round, 2, 2, 0, low)
+        weave_left(gpsimd_round, slice(0, 3), slice(0, 3), 0, low)
+        for first, width in halves:
+            weave_right(first, width)
+        v2_w = held("v2_w", [P, S2], U32)
+        nc.vector.tensor_copy(out=v2_w[:], in_=tab2_w[:].bitcast(U32).indirect(list2[:]))
 
         page_q = held("page_q", [P, T2], U32)
         page_s = held("page_s", [P, T2], U8)
@@ -396,14 +420,13 @@ def tile_list_lifeboat_heun_scores_kernel(
             cols = slice(first, first + width)
             nc.vector.quantize_mx(out=page_q[:, cols].bitcast(FP8X4), scales=page_s[:, cols], in_=woven_page(first, width).rearrange("p n t -> p (n t)"))
 
+        cuts = [(0, N), (N, N), (2 * N, N), (3 * N, Q), (3 * N + Q, P), (T2 - P, P)]
         round_plane(gpsimd_round, 3, 0, low)
-        round_plane(nc.scalar.copy, 3, 2 * N, N)
-        round_plane(nc.scalar.copy, 3, 3 * N, Q)
-        round_plane(nc.scalar.copy, 3, 3 * N + Q, P)
-        round_plane(nc.scalar.copy, 3, T2 - P, P)
-        nc.vector.tensor_copy(out=flat[:, 1, :], in_=pages[3][:, low:side])
-        nc.vector.tensor_copy(out=woven_page(low, side - low)[:, :, 2:], in_=flat[:].rearrange("p e n -> p n e"))
-        cuts = [(2 * N, N), (0, N), (N, N), (3 * N, Q), (3 * N + Q, P), (T2 - P, P)]
+        round_plane(nc.scalar.copy, 3, side, 2 * N - side)
+        for first, width in cuts[2:]:
+            round_plane(nc.scalar.copy, 3, first, width)
+        round_left(nc.vector.tensor_copy, 3, 1, low, low)
+        weave_left(nc.vector.tensor_copy, slice(2, 4), slice(0, 2), low, low)
         for first, width in cuts:
             quantise_page(first, width)
 
@@ -420,14 +443,14 @@ def tile_list_lifeboat_heun_scores_kernel(
             copy(out=scores[:, base : base + total], in_=acc[:, :total])
 
         for n in range(boats):
-            scores = held("scores%d" % (n % 3), [P, T2], F32)
+            scores = held(("scores0", "tab_w", "scores2")[n % 3], [P, T2], F32)
             if n == 0:
                 for i in range(4):
                     score(i, scores, n, cuts[i : i + 1], nc.scalar.copy)
                 score(4, scores, n, cuts[4:], nc.vector.tensor_copy)
             else:
-                for i, c in enumerate((2, 0, 1, 3)):
-                    score((5 + 4 * (n - 1) + i) % 8, scores, n, [(c * N, N)], nc.scalar.copy)
+                for i, c in enumerate((0, 1, 2, 3)):
+                    score((0, 1, 5, 6)[i], scores, n, [(c * N, N)], nc.scalar.copy)
             pieces = [(0, PICK)] if n < boats - 1 else [(0, N), (N, N - P), (PICK - P, P)]
             for first, width in pieces:
                 picked = held(("w_raw0", "w_raw1", "wgs0")[n] if n < 3 else "picked%d" % first, [P, width], F32)

@@ -320,7 +320,7 @@ def tile_list_lifeboat_heun_scores_kernel(
         pair = held("pair", [P, 2, Q], F32)
         nc.gpsimd.tensor_tensor(pair[:], up2[:, rows, :], up1[:, rows, :], ADD)
         third = held("values2_0", [P, Q], F32)
-        last = held("values_last", [P, S], F32)
+        last = held("values_last", [P, S - Q], F32)
         nc.gpsimd.tensor_tensor(third[:], pair[:, 0, :], weights_of(2, 0, Q), MULT)
         nc.gpsimd.tensor_tensor(last[:, :Q], pair[:, 1, :], weights_of(3, 0, Q), MULT)
         put(third[:], 2, 0, Q)
@@ -366,14 +366,17 @@ def tile_list_lifeboat_heun_scores_kernel(
                 second_slope(b)
             for t in range(3):
                 piece((7, 6, 2)[t] if q == 2 else (3, 4, 5)[t], t, q * Q, Q)
-        staged = held("v2_w", [P, N], F32)
-        make_values(last[:, N:], 7, 3, N, N, staged[:])
-        put(last[:], 3, 0, S)
+        staged = held("flats", [P, Q], F32)
+        make_values(last[:, N:], 7, 3, N, Q, staged[:])
+        put(last[:], 3, 0, S - Q)
+        staged = held("v2_w", [P, Q], F32)
+        nc.scalar.activation(staged[:], slope_sum(6, 3, S - Q, Q), COPY, scale=half_gain[:, 3:4])
 
         low = 3 * P
-        side = 2 * low
+        side = N + low
         page_bf = held("tab_w", [P, T2, PACK], BF16)
-        left = held("wgs%d" % N, [P, 3, side], BF16)
+        flats = held("flats", [P, 5, low], BF16)
+        front = held("values2_%d" % N, [P, 3, Q], BF16)
         right = held("half_gain", [P, 3, T2 - side], BF16)
 
         def woven_page(first, width):
@@ -382,14 +385,14 @@ def tile_list_lifeboat_heun_scores_kernel(
         def round_plane(copy, t, first, width):
             copy(out=woven_page(first, width)[:, :, t], in_=pages[t][:, first : first + width])
 
-        def round_left(copy, t, row, first, width):
-            copy(out=left[:, row, first : first + width], in_=pages[t][:, first : first + width])
+        def round_left(rows, t, first, width):
+            gpsimd_round(rows[:, t, :width], pages[t][:, first : first + width])
 
         def round_right(t, first, width):
             nc.scalar.copy(out=right[:, t, first - side : first - side + width], in_=pages[t][:, first : first + width])
 
-        def weave_left(copy, planes, rows, first, width):
-            copy(out=woven_page(first, width)[:, :, planes], in_=left[:, rows, first : first + width].rearrange("p t n -> p n t"))
+        def weave_left(rows, first, width):
+            gpsimd_round(woven_page(first, width)[:, :, :3], rows[:, :, :width].rearrange("p t n -> p n t"))
 
         def weave_right(first, width):
             nc.scalar.copy(
@@ -402,12 +405,22 @@ def tile_list_lifeboat_heun_scores_kernel(
             round_right(t, side, T2 - side)
         for first, width in halves:
             round_right(2, first, width)
+        shares = [(front[:], 0, Q), (flats[:, 2:, :], Q, Q), (flats[:, :3, :], N, low)]
         for t in range(2):
-            round_left(gpsimd_round, t, t, 0, side)
-        weave_left(gpsimd_round, slice(0, 2), slice(0, 2), low, low)
-        round_left(gpsimd_round, 2, 0, low, low)
-        round_left(gpsimd_round, 2, 2, 0, low)
-        weave_left(gpsimd_round, slice(0, 3), slice(0, 3), 0, low)
+            for rows, first, width in shares:
+                round_left(rows, t, first, width)
+        for rows, first, width in shares[:2]:
+            round_left(rows, 2, first, width)
+        for rows, first, width in shares[:2]:
+            weave_left(rows, first, width)
+        values = held("values2_%d" % N, [P, Q], F32)
+        nc.gpsimd.tensor_tensor(values[:], staged[:], weights_of(3, S - Q, Q), MULT)
+        put(values[:], 3, S - Q, Q)
+        parts = [(flats[:, :3, lo : lo + low // 2], N + lo, low // 2) for lo in (0, low // 2)]
+        for rows, first, width in parts:
+            round_left(rows, 2, first, width)
+        for rows, first, width in parts:
+            weave_left(rows, first, width)
         for first, width in halves:
             weave_right(first, width)
         v2_w = held("v2_w", [P, S2], U32)
@@ -421,12 +434,11 @@ def tile_list_lifeboat_heun_scores_kernel(
             nc.vector.quantize_mx(out=page_q[:, cols].bitcast(FP8X4), scales=page_s[:, cols], in_=woven_page(first, width).rearrange("p n t -> p (n t)"))
 
         cuts = [(0, N), (N, N), (2 * N, N), (3 * N, Q), (3 * N + Q, P), (T2 - P, P)]
-        round_plane(gpsimd_round, 3, 0, low)
+        round_plane(gpsimd_round, 3, N, low)
         round_plane(nc.scalar.copy, 3, side, 2 * N - side)
         for first, width in cuts[2:]:
             round_plane(nc.scalar.copy, 3, first, width)
-        round_left(nc.vector.tensor_copy, 3, 1, low, low)
-        weave_left(nc.vector.tensor_copy, slice(2, 4), slice(0, 2), low, low)
+        round_plane(nc.vector.tensor_copy, 3, 0, N)
         for first, width in cuts:
             quantise_page(first, width)
 
@@ -445,12 +457,11 @@ def tile_list_lifeboat_heun_scores_kernel(
         for n in range(boats):
             scores = held(("scores0", "tab_w", "scores2")[n % 3], [P, T2], F32)
             if n == 0:
-                for i in range(4):
-                    score(i, scores, n, cuts[i : i + 1], nc.scalar.copy)
-                score(4, scores, n, cuts[4:], nc.vector.tensor_copy)
+                for i, cut in enumerate(cuts):
+                    score(i, scores, n, [cut], nc.scalar.copy if i < 3 else nc.vector.tensor_copy)
             else:
-                for i, c in enumerate((0, 1, 2, 3)):
-                    score((0, 1, 5, 6)[i], scores, n, [(c * N, N)], nc.scalar.copy)
+                for i, c in enumerate((3, 0, 1, 2)):
+                    score((6, 3, 4, 5)[i], scores, n, [(c * N, N)], nc.scalar.copy)
             pieces = [(0, PICK)] if n < boats - 1 else [(0, N), (N, N - P), (PICK - P, P)]
             for first, width in pieces:
                 picked = held(("w_raw0", "w_raw1", "wgs0")[n] if n < 3 else "picked%d" % first, [P, width], F32)

@@ -38,7 +38,8 @@ def tile_list_lifeboat_heun_scores_kernel(
         psum = ctx.enter_context(tc.psum_pool(name="psum", bufs=1))
 
         def held(name, shape, dtype):
-            return keep.tile(shape, dtype, name=name, align_bytes=64)
+            wide = name[:4] in ("tab_", "tab2", "w_ra", "page", "reac", "wgs0", "wgs2", "wgs5", "pick")
+            return keep.tile(shape, dtype, name=name, align_bytes=256 if wide else 64)
 
         def bank(b):
             return psum.tile([P, N], F32, name="bank%d" % b)
@@ -68,7 +69,7 @@ def tile_list_lifeboat_heun_scores_kernel(
         tab_s = held("tab_s", [P, T], U8)
         tab2_w = held("tab2_w", [P, T3], I32)
         tab2_s = held("tab2_s", [P, T3], U8)
-        w_raw = [held("w_raw%d" % u, [P, PACK, Q], F32) for u in range(2)]
+        w_raw = [held("w_raw%d" % u, [P, 2, H], F32) for u in range(2)]
         wf_raw = held("wf_raw", [P, 2 * H], U8)
         wf_s_raw = held("wf_s_raw", [P, H], U8)
         gain_sb = held("gain_sb", [P, PACK], F32)
@@ -111,7 +112,7 @@ def tile_list_lifeboat_heun_scores_kernel(
         nc.sync.dma_start(out=tab_w[:, T // 4 :], in_=words_of(tab_words)[:, T // 4 :])
         load_scale_rows(wf_s_raw, wf_scales)
         for u in range(2):
-            nc.sync.dma_start(out=w_raw[u][:], in_=w_rows[:, :, u * Q : (u + 1) * Q])
+            nc.sync.dma_start(out=w_raw[u][:], in_=w_rows[:, 2 * u : 2 * u + 2, :])
         v_spread = held("v_spread", [P, S], U8)
         v2_spread = held("v2_spread", [P, S2], U8)
         nc.vector.tensor_copy(out=v_spread[:], in_=tab_s[:].indirect(list1[:]))
@@ -150,11 +151,10 @@ def tile_list_lifeboat_heun_scores_kernel(
         wq = held("wq", [P, H], U32)
         wq_s = held("wq_s", [P, H], U8)
 
-        def round_w(copy, part, u):
-            half = slice(part * P // 2, (part + 1) * P // 2)
+        def round_w(copy, part, u, cols):
             copy(
-                out=w_bf[u][:, :, half, :].rearrange("p t m j -> p m t j"),
-                in_=w_raw[part][:].rearrange("p j (m t) -> p m t j", t=PACK)[:, :, 2 * u : 2 * u + 2, :],
+                out=w_bf[u][:, :, cols, 2 * part : 2 * part + 2].rearrange("p t m j -> p m t j"),
+                in_=w_raw[part][:].rearrange("p j (m t) -> p m t j", t=PACK)[:, cols, 2 * u : 2 * u + 2, :],
             )
 
         def quantise_w(u):
@@ -162,8 +162,9 @@ def tile_list_lifeboat_heun_scores_kernel(
             nc.vector.quantize_mx(out=wq[:, cols].bitcast(FP8X4), scales=wq_s[:, cols], in_=w_bf[u][:].rearrange("p t m j -> p (t m j)"))
 
         for part in range(2):
-            round_w(nc.vector.tensor_copy, part, 0)
-            round_w(nc.scalar.copy, part, 1)
+            round_w(nc.vector.tensor_copy, part, 0, slice(0, P))
+            round_w(nc.vector.tensor_copy, part, 1, slice(0, P // 4))
+            round_w(nc.scalar.copy, part, 1, slice(P // 4, P))
         for u in range(2):
             quantise_w(u)
         v_w[1] = held("w_bf1", [P, N], U32)

@@ -38,7 +38,7 @@ def tile_list_lifeboat_heun_scores_kernel(
         psum = ctx.enter_context(tc.psum_pool(name="psum", bufs=1))
 
         def held(name, shape, dtype):
-            wide = name[:4] in ("tab_", "tab2", "w_ra", "page", "reac", "wgs0", "wgs2", "wgs5", "pick")
+            wide = name[:4] in ("tab_", "tab2", "w_ra", "page", "reac", "wgs0", "wgs2", "wgs5", "pick", "wf_r")
             return keep.tile(shape, dtype, name=name, align_bytes=256 if wide else 64)
 
         def bank(b):
@@ -49,11 +49,11 @@ def tile_list_lifeboat_heun_scores_kernel(
                 nc.sync.dma_start(out=plane[r:P:32, :].bitcast(I32), in_=rows[0, r:16:4, :].bitcast(I32))
 
         def load_spread(plane, rows):
-            nc.sync.dma_start(out=plane[0:P:8, :].bitcast(I32), in_=rows[0].bitcast(I32))
+            nc.sync.dma_start(out=plane[0 : 16 * 7 : 7, :].bitcast(I32), in_=rows[0].bitcast(I32))
 
         def move_scale_rows(plane, spread):
             for r in range(4):
-                nc.sync.dma_start(out=plane[r:P:32, :].bitcast(I32), in_=spread[8 * r : P : 32, :].bitcast(I32))
+                nc.sync.dma_start(out=plane[r:P:32, :].bitcast(I32), in_=spread[7 * r : 16 * 7 : 4 * 7, :].bitcast(I32))
 
         def words_of(table):
             return table[0].rearrange("p n i -> p (n i)").bitcast(I32)
@@ -103,8 +103,8 @@ def tile_list_lifeboat_heun_scores_kernel(
                     in_=wgs_rows[:, :, first : first + Q],
                 )
 
-        nc.sync.dma_start(list1[:], offs)
         nc.sync.dma_start(out=tab_w[:, : T // 4], in_=words_of(tab_words)[:, : T // 4])
+        nc.sync.dma_start(list1[:], offs)
         nc.sync.dma_start(out=wf_raw[:].bitcast(I32), in_=wf_words[0].bitcast(I32))
         load_spread(tab_s, tab_scales)
         nc.sync.dma_start(list2[:], offs2)
@@ -293,8 +293,7 @@ def tile_list_lifeboat_heun_scores_kernel(
         def upright_second(z_bank, planes):
             z = bank(z_bank)
             for e, t in enumerate(planes):
-                for b in range(2):
-                    upright(z[:, e * Q + b * P : e * Q + (b + 1) * P], t, FP4X4, *entries(b), e == 0 and b == 0, False)
+                upright(z[:, e * Q : (e + 1) * Q], t, FP4X4, v_w[0][:, :Q], v_s[:, :Q], e == 0, False)
                 upright(z[:, e * Q : (e + 1) * Q], t, FP8X4, v_w[0][:, :Q], v_s[:, :Q], False, False)
             for e, t in enumerate(planes):
                 upright(z[:, e * Q : (e + 1) * Q], t, FP8X4, d1[0][:], d1_s[0][:], False, t == planes[-1])
@@ -302,8 +301,7 @@ def tile_list_lifeboat_heun_scores_kernel(
             nc.scalar.activation(up2[:, rows, :], z[:, : len(planes) * Q].rearrange("p (e n) -> p e n", n=Q), TANH)
             return rows
 
-        for t in range(2):
-            upright_second(4 + t, [t])
+        upright_second(4, [0, 1])
         first_step(3)
         both = held("pair", [P, 2, Q], F32)
         nc.vector.tensor_tensor(both[:], up2[:, :2, :], up1[:, :2, :], ADD)
@@ -361,12 +359,16 @@ def tile_list_lifeboat_heun_scores_kernel(
         quantise_step(3)
         make_values(last[:, Q:N], 6, 3, Q, Q)
         for q in (2, 3):
+            sum_banks = (7, 6, 2) if q == 2 else (3, 4, 5)
             for b in (2 * q, 2 * q + 1):
                 open_second(b)
                 close_second(b)
-                second_slope(b)
-            for t in range(3):
-                piece((7, 6, 2)[t] if q == 2 else (3, 4, 5)[t], t, q * Q, Q)
+                second_slope(b, slice(0, 1))
+            piece(sum_banks[0], 0, q * Q, Q)
+            for b in (2 * q, 2 * q + 1):
+                second_slope(b, slice(1, PACK))
+            for t in (1, 2):
+                piece(sum_banks[t], t, q * Q, Q)
         staged = held("flats", [P, Q], F32)
         make_values(last[:, N:], 7, 3, N, Q, staged[:])
         put(last[:], 3, 0, S - Q)

from contextlib import ExitStack

import concourse.mybir as mybir
from concourse.masks import make_identity

K, T, S, H, T2, S2, T3, PICK = 512, 4096, 1024, 512, 2048, 512, 2048, 1024
FLOPS = 2 * (5 * K * H * S + H * S2 * T2)

F32 = mybir.dt.float32
BF16 = mybir.dt.bfloat16
I32 = mybir.dt.int32
U32 = mybir.dt.uint32
U16 = mybir.dt.uint16
U8 = mybir.dt.uint8
FP8X4 = mybir.dt.float8_e4m3fn_x4
FP4X4 = mybir.dt.float4_e2m1fn_x4
MULT = mybir.AluOpType.mult
ADD = mybir.AluOpType.add
TANH = mybir.ActivationFunctionType.Tanh
COPY = mybir.ActivationFunctionType.Copy

P = 128
PACK = 4
N = 512
Q = N // 2
PER_COL = 16


def tile_list_lifeboat_heun_scores_kernel(
    tc, tab_words, tab_scales, offs, tab2_words, tab2_scales, offs2, offs3, offs4,
    w, wf_words, wf_scales, gain, page0, wgs, reach, out,
):
    nc = tc.nc
    boats = S2 // P

    with ExitStack() as ctx:
        keep = ctx.enter_context(tc.tile_pool(name="keep", bufs=1))
        psum = ctx.enter_context(tc.psum_pool(name="psum", bufs=1))

        def held(name, shape, dtype):
            wide = name[:4] in ("tab_", "tab2", "w_ra", "page", "reac", "wgs0", "wgs2", "wgs5", "pick", "wf_r")
            return keep.tile(shape, dtype, name=name, align_bytes=256 if wide else 64)

        def bank(b):
            return psum.tile([P, N], F32, name="bank%d" % b)

        def load_scale_rows(plane, rows):
            for r in range(4):
                nc.sync.dma_start(out=plane[r:P:32, :].bitcast(I32), in_=rows[0, r:16:4, :].bitcast(I32))

        def load_spread(plane, rows):
            nc.sync.dma_start(out=plane[0 : 16 * 7 : 7, :].bitcast(I32), in_=rows[0].bitcast(I32))

        def move_scale_rows(plane, spread):
            for r in range(4):
                nc.sync.dma_start(out=plane[r:P:32, :].bitcast(I32), in_=spread[7 * r : 16 * 7 : 4 * 7, :].bitcast(I32))

        def words_of(table):
            return table[0].rearrange("p n i -> p (n i)").bitcast(I32)

        def columns(lists, first, count):
            return lists[:, first // PER_COL : (first + count) // PER_COL]

        list1 = held("list1", [P, S // PER_COL], U16)
        list2 = held("list2", [P, S2 // PER_COL], U16)
        list3 = held("list3", [P, S // PER_COL], U16)
        list4 = held("list4", [P, PICK // PER_COL], U16)
        tab_w = held("tab_w", [P, T], I32)
        tab_s = held("tab_s", [P, T], U8)
        tab2_w = held("tab2_w", [P, T3], I32)
        tab2_s = held("tab2_s", [P, T3], U8)
        w_raw = [held("w_raw%d" % u, [P, 2, H], F32) for u in range(2)]
        wf_raw = held("wf_raw", [P, 2 * H], U8)
        wf_s_raw = held("wf_s_raw", [P, H], U8)
        gain_sb = held("gain_sb", [P, PACK], F32)
        pages = [held("page%d" % t, [P, T2], F32) for t in range(PACK)]
        wgs_cuts = [(0, Q), (Q, Q), (N, N)]
        wgs_sb = {first: held("wgs%d" % first, [P, PACK, width], F32) for first, width in wgs_cuts}
        reach_sb = [held("reach%d" % n, [P, PICK], F32) for n in range(boats)]

        nc.gpsimd.memset(tab_s[:, : T // 2].bitcast(I32), 0)
        nc.vector.memset(tab_s[:, T // 2 :].bitcast(I32), 0)
        nc.vector.memset(tab2_s[:].bitcast(I32), 0)
        nc.vector.memset(wf_s_raw[:].bitcast(I32), 0)

        v_s = held("v_s", [P, S], U8)
        v2_s = held("v2_s", [P, S2], U8)
        nc.vector.memset(v_s[:].bitcast(I32), 0)
        nc.vector.memset(v2_s[:].bitcast(I32), 0)

        identity = held("identity", [P, P], F32)
        make_identity(nc, identity[:])

        page_rows = page0.rearrange("(p t) c -> t p c", t=PACK)
        wgs_rows = wgs.rearrange("(m t) j -> m t j", t=PACK)
        w_rows = w.rearrange("(p j) c -> p j c", j=PACK)

        def load_wgs(first):
            base = min(first, N)
            for q in (0, 2, 1, 3):
                nc.sync.dma_start(
                    out=wgs_sb[base][32 * q : 32 * q + 32, :, first - base : first - base + Q],
                    in_=wgs_rows[:, :, first : first + Q],
                )

        nc.sync.dma_start(out=tab_w[:, : T // 4], in_=words_of(tab_words)[:, : T // 4])
        nc.sync.dma_start(list1[:], offs)
        nc.sync.dma_start(out=wf_raw[:].bitcast(I32), in_=wf_words[0].bitcast(I32))
        load_spread(tab_s, tab_scales)
        nc.sync.dma_start(list2[:], offs2)
        load_spread(tab2_s, tab2_scales)
        nc.sync.dma_start(out=tab_w[:, T // 4 :], in_=words_of(tab_words)[:, T // 4 :])
        load_scale_rows(wf_s_raw, wf_scales)
        for u in range(2):
            nc.sync.dma_start(out=w_raw[u][:], in_=w_rows[:, 2 * u : 2 * u + 2, :])
        v_spread = held("v_spread", [P, S], U8)
        v2_spread = held("v2_spread", [P, S2], U8)
        nc.vector.tensor_copy(out=v_spread[:], in_=tab_s[:].indirect(list1[:]))
        nc.vector.tensor_copy(out=v2_spread[:], in_=tab2_s[:].indirect(list2[:]))
        move_scale_rows(v_s, v_spread)
        nc.sync.dma_start(out=gain_sb[:], in_=gain.rearrange("(p t) -> p t", t=PACK))
        nc.sync.dma_start(out=pages[0][:], in_=page_rows[0])
        load_wgs(0)
        nc.sync.dma_start(list3[:], offs3)
        for t in range(1, PACK - 1):
            nc.sync.dma_start(out=pages[t][:], in_=page_rows[t])
        load_wgs(Q)
        load_wgs(2 * Q)
        load_wgs(3 * Q)
        nc.sync.dma_start(out=pages[PACK - 1][:], in_=page_rows[PACK - 1])
        nc.sync.dma_start(out=tab2_w[:], in_=words_of(tab2_words))
        move_scale_rows(v2_s, v2_spread)
        nc.sync.dma_start(list4[:], offs4)
        for n in range(boats):
            nc.sync.dma_start(out=reach_sb[n][:], in_=reach[n * P : (n + 1) * P, :])

        v_w = {0: held("v_w0", [P, N], U32)}
        wf = held("wf", [P, 2 * H], U8)
        wf_s = held("wf_s", [P, H], U8)
        nc.vector.tensor_copy(
            out=wf[:].bitcast(U16).rearrange("p (t m) -> p t m", t=PACK),
            in_=wf_raw[:].bitcast(U16).rearrange("p (m t) -> p t m", t=PACK),
        )
        nc.vector.tensor_copy(out=v_w[0][:], in_=tab_w[:].bitcast(U32).indirect(columns(list1, 0, N)))
        nc.gpsimd.tensor_copy(
            out=wf_s[:].rearrange("p (t m) -> p t m", t=PACK),
            in_=wf_s_raw[:].rearrange("p (m t) -> p t m", t=PACK),
        )

        w_bf = [held("w_bf%d" % u, [P, 2, P, PACK], BF16) for u in range(2)]
        wq = held("wq", [P, H], U32)
        wq_s = held("wq_s", [P, H], U8)

        def round_w(copy, part, u, cols):
            copy(
                out=w_bf[u][:, :, cols, 2 * part : 2 * part + 2].rearrange("p t m j -> p m t j"),
                in_=w_raw[part][:].rearrange("p j (m t) -> p m t j", t=PACK)[:, cols, 2 * u : 2 * u + 2, :],
            )

        def quantise_w(u):
            cols = slice(u * Q, (u + 1) * Q)
            nc.vector.quantize_mx(out=wq[:, cols].bitcast(FP8X4), scales=wq_s[:, cols], in_=w_bf[u][:].rearrange("p t m j -> p (t m j)"))

        for part in range(2):
            round_w(nc.vector.tensor_copy, part, 0, slice(0, P))
            round_w(nc.vector.tensor_copy, part, 1, slice(0, P // 4))
            round_w(nc.scalar.copy, part, 1, slice(P // 4, P))
        for u in range(2):
            quantise_w(u)
        v_w[1] = held("w_bf1", [P, N], U32)
        nc.vector.tensor_copy(out=v_w[1][:], in_=tab_w[:].bitcast(U32).indirect(columns(list1, N, N)))
        half_gain = held("half_gain", [P, PACK], F32)
        nc.gpsimd.tensor_scalar(half_gain[:], gain_sb[:], 0.5, 0.0, MULT, ADD)

        def entries(b):
            h, lo = divmod(b * P, N)
            return v_w[h][:, lo : lo + P], v_s[:, b * P : (b + 1) * P]

        def mx(acc, left, fmt, codes, scales, start, stop):
            nc.tensor.matmul_mx(
                out=acc, lhsT=left[0].bitcast(FP8X4), lhsT_scale=left[1],
                rhs=codes.bitcast(fmt), rhs_scale=scales, start=start, stop=stop,
            )

        def forcing_pass(acc, b):
            mx(acc[:], entries(b), FP4X4, wf[:], wf_s[:], True, False)

        def drift_pass(acc, left, stop, first=0, width=N):
            cols = slice(first, first + width)
            mx(acc[:, cols], left, FP8X4, wq[:, cols], wq_s[:, cols], False, stop)

        blocks = S // P
        t1 = {b: held("t1_%d" % b, [P, PACK, P], F32) for b in range(2, blocks)}
        t2 = {b: held("t2_%d" % b, [P, PACK, P], F32) for b in range(2, blocks)}
        woven = {q: held("woven%d" % q, [P, Q, PACK], BF16) for q in range(3)}
        d1 = {q: held("d1_%d" % q, [P, Q], U32) for q in (0, 1, 3)}
        d1_s = [held("d1_s%d" % q, [P, Q], U8) for q in range(S // Q)]
        z2 = {}

        def by_plane(acc):
            return acc[:].rearrange("p (t m) -> p t m", t=PACK)

        def first_slope(b, z_bank=None):
            z1 = bank(b % 2 if z_bank is None else z_bank)
            forcing_pass(z1, b)
            drift_pass(z1, entries(b), True)
            nc.scalar.activation(t1[b][:], by_plane(z1), TANH)

        def first_step(b):
            back = bank(2 + b % 2)
            for t in range(PACK):
                nc.tensor.transpose(back[:, t * P : (t + 1) * P], t1[b][:, t, :], identity[:])
            q, lo = divmod(b * P, Q)
            nc.vector.tensor_tensor(
                woven[q][:, lo : lo + P, :], back[:].rearrange("p (t n) -> p n t", t=PACK),
                gain_sb[:].unsqueeze(1).to_broadcast([P, P, PACK]), MULT,
            )

        def quantise_step(q, lo=0, width=Q):
            cols = slice(lo, lo + width)
            nc.vector.quantize_mx(out=d1[q][:, cols].bitcast(FP8X4), scales=d1_s[q][:, cols], in_=woven[q][:, cols, :].rearrange("p n t -> p (n t)"))

        def open_second(b):
            z2[b] = bank(4 + b % 2 if b < 6 else (6, 2)[b % 2])
            forcing_pass(z2[b], b)
            drift_pass(z2[b], entries(b), False)

        def close_second(b):
            q, lo = divmod(b * P, Q)
            drift_pass(z2[b], (d1[q][:, lo : lo + P], d1_s[q][:, lo : lo + P]), True)

        def second_slope(b, planes=slice(0, PACK)):
            nc.scalar.activation(t2[b][:, planes, :], by_plane(z2[b])[:, planes, :], TANH)

        def slope_sum(sum_bank, t, first, width):
            total = bank(sum_bank)
            here = range(first // P, (first + width) // P)
            for k, slopes in enumerate((t1, t2)):
                for b in here:
                    lo = b * P - first
                    nc.tensor.matmul(
                        total[:, lo : lo + P], slopes[b][:, t, :], identity[:],
                        start=k == 0 and b == here[0], stop=k == 1 and b == here[-1], is_transpose=True,
                    )
            return total[:, :width]

        def weights_of(t, first, width):
            base = min(first, N)
            return wgs_sb[base][:, t, first - base : first - base + width]

        def make_values(values, sum_bank, t, first, width, staged=None):
            staged = values if staged is None else staged
            nc.scalar.activation(staged, slope_sum(sum_bank, t, first, width), COPY, scale=half_gain[:, t : t + 1])
            nc.gpsimd.tensor_tensor(values, staged, weights_of(t, first, width), MULT)

        def put(values, t, first, width):
            nc.vector.tensor_copy(pages[t][:].indirect(columns(list3, first, width)), values)

        def piece(sum_bank, t, first, width):
            values = held("values%d_%d" % (t, first), [P, width], F32)
            make_values(values[:], sum_bank, t, first, width)
            put(values[:], t, first, width)

        def upright(acc, t, fmt, codes, scales, start, stop):
            size = 2 if fmt == FP4X4 else 1
            weights, weight_scales = (wf, wf_s) if fmt == FP4X4 else (wq, wq_s)
            nc.tensor.matmul_mx(
                out=acc, lhsT=weights[:, size * t * P : size * (t + 1) * P].bitcast(fmt), lhsT_scale=weight_scales[:, t * P : (t + 1) * P],
                rhs=codes.bitcast(FP8X4), rhs_scale=scales, start=start, stop=stop,
            )

        up1 = held("up1", [P, PACK, Q], F32)
        up2 = held("up2", [P, PACK, Q], F32)
        early = [bank(b) for b in range(2)]
        for b in range(2):
            for t in range(PACK):
                upright(early[b][:, t * P : (t + 1) * P], t, FP4X4, *entries(b), t == 0, False)
        for b in range(2):
            cols = slice(b * P, (b + 1) * P)
            for t in range(PACK):
                upright(early[b][:, t * P : (t + 1) * P], t, FP8X4, *entries(b), False, t == PACK - 1)
            nc.scalar.activation(up1[:, :, cols], by_plane(early[b]), TANH)
            nc.vector.tensor_tensor(
                woven[0][:, cols, :].rearrange("p (c i) t -> p c t i", i=4), up1[:, :, cols].rearrange("p t (c i) -> p c t i", i=4),
                gain_sb[:].unsqueeze(1).unsqueeze(3).to_broadcast([P, P // 4, PACK, 4]), MULT,
            )
        for b in range(2):
            quantise_step(0, b * P, P)
        first_slope(2, 7)
        first_step(2)
        first_slope(3, 0)

        def upright_second(z_bank, planes):
            z = bank(z_bank)
            for e, t in enumerate(planes):
                upright(z[:, e * Q : (e + 1) * Q], t, FP4X4, v_w[0][:, :Q], v_s[:, :Q], e == 0, False)
                upright(z[:, e * Q : (e + 1) * Q], t, FP8X4, v_w[0][:, :Q], v_s[:, :Q], False, False)
            for e, t in enumerate(planes):
                upright(z[:, e * Q : (e + 1) * Q], t, FP8X4, d1[0][:], d1_s[0][:], False, t == planes[-1])
            rows = slice(planes[0], planes[-1] + 1)
            nc.scalar.activation(up2[:, rows, :], z[:, : len(planes) * Q].rearrange("p (e n) -> p e n", n=Q), TANH)
            return rows

        upright_second(4, [0, 1])
        first_step(3)
        both = held("pair", [P, 2, Q], F32)
        nc.vector.tensor_tensor(both[:], up2[:, :2, :], up1[:, :2, :], ADD)
        quantise_step(1)
        values = [held("values%d_0" % t, [P, Q], F32) for t in range(2)]
        for t in range(2):
            nc.vector.scalar_tensor_tensor(values[t][:], both[:, t, :], half_gain[:, t : t + 1], weights_of(t, 0, Q), MULT, MULT)
        for t in range(2):
            put(values[t][:], t, 0, Q)
        for t in (2, 3):
            nc.gpsimd.tensor_scalar(weights_of(t, 0, Q), weights_of(t, 0, Q), half_gain[:, t : t + 1], 0.0, MULT, ADD)
        for b in (4, 5):
            first_slope(b, 1 - b % 2)
        rows = upright_second(6, [2, 3])
        pair = held("pair", [P, 2, Q], F32)
        nc.gpsimd.tensor_tensor(pair[:], up2[:, rows, :], up1[:, rows, :], ADD)
        third = held("values2_0", [P, Q], F32)
        last = held("values_last", [P, S - Q], F32)
        nc.gpsimd.tensor_tensor(third[:], pair[:, 0, :], weights_of(2, 0, Q), MULT)
        nc.gpsimd.tensor_tensor(last[:, :Q], pair[:, 1, :], weights_of(3, 0, Q), MULT)
        put(third[:], 2, 0, Q)

        def gpsimd_round(out, in_):
            nc.gpsimd.tensor_scalar(out, in_, 1.0, 0.0, MULT, ADD)

        def late_step(q):
            flat = held("flat%d" % q, [P, PACK, Q], BF16)
            for u in range(2):
                back = bank(2 + u)
                for e in range(2):
                    for b in range(2):
                        nc.tensor.transpose(back[:, e * Q + b * P : e * Q + (b + 1) * P], t1[2 * q + b][:, 2 * u + e, :], identity[:])
                for e in range(2):
                    t = 2 * u + e
                    nc.scalar.activation(flat[:, t, :], back[:, e * Q : (e + 1) * Q], COPY, scale=gain_sb[:, t : t + 1])
            gpsimd_round(woven[q][:], flat[:].rearrange("p t n -> p n t"))

        for b in (2, 3):
            open_second(b)
            close_second(b)
            second_slope(b)
        late_step(2)
        d1[2] = held("values2_0", [P, Q], U32)
        quantise_step(2)
        piece(7, 0, Q, Q)
        for b in (6, 7):
            first_slope(b, 1 - b % 2)
        piece(6, 1, Q, Q)
        staged = held("woven3", [P, Q], F32)
        values = held("values2_%d" % Q, [P, Q], F32)
        make_values(values[:], 7, 2, Q, Q, staged[:])
        put(values[:], 2, Q, Q)
        woven[3] = held("woven3", [P, Q, PACK], BF16)
        late_step(3)
        quantise_step(3)
        make_values(last[:, Q:N], 6, 3, Q, Q)
        for q in (2, 3):
            sum_banks = (7, 6, 2) if q == 2 else (3, 4, 5)
            for b in (2 * q, 2 * q + 1):
                open_second(b)
                close_second(b)
                second_slope(b, slice(0, 1))
            piece(sum_banks[0], 0, q * Q, Q)
            for b in (2 * q, 2 * q + 1):
                second_slope(b, slice(1, PACK))
            for t in (1, 2):
                piece(sum_banks[t], t, q * Q, Q)
        staged = held("flats", [P, Q], F32)
        make_values(last[:, N:], 7, 3, N, Q, staged[:])
        put(last[:], 3, 0, S - Q)
        staged = held("v2_w", [P, Q], F32)
        nc.scalar.activation(staged[:], slope_sum(6, 3, S - Q, Q), COPY, scale=half_gain[:, 3:4])

        low = 3 * P
        side = N + low
        page_bf = held("tab_w", [P, T2, PACK], BF16)
        flats = held("flats", [P, 5, low], BF16)
        front = held("values2_%d" % N, [P, 3, Q], BF16)
        right = held("half_gain", [P, 3, T2 - side], BF16)

        def woven_page(first, width):
            return page_bf[:, first : first + width, :]

        def round_plane(copy, t, first, width):
            copy(out=woven_page(first, width)[:, :, t], in_=pages[t][:, first : first + width])

        def round_left(rows, t, first, width):
            gpsimd_round(rows[:, t, :width], pages[t][:, first : first + width])

        def round_right(t, first, width):
            nc.scalar.copy(out=right[:, t, first - side : first - side + width], in_=pages[t][:, first : first + width])

        def weave_left(rows, first, width):
            gpsimd_round(woven_page(first, width)[:, :, :3], rows[:, :, :width].rearrange("p t n -> p n t"))

        def weave_right(first, width):
            nc.scalar.copy(
                out=woven_page(first, width)[:, :, :3].rearrange("p (c i) t -> p c t i", i=2),
                in_=right[:, :, first - side : first - side + width].rearrange("p t (c i) -> p c t i", i=2),
            )

        halves = [(side, (T2 - side) // 2), ((T2 + side) // 2, (T2 - side) // 2)]
        for t in range(2):
            round_right(t, side, T2 - side)
        for first, width in halves:
            round_right(2, first, width)
        shares = [(front[:], 0, Q), (flats[:, 2:, :], Q, Q), (flats[:, :3, :], N, low)]
        for t in range(2):
            for rows, first, width in shares:
                round_left(rows, t, first, width)
        for rows, first, width in shares[:2]:
            round_left(rows, 2, first, width)
        for rows, first, width in shares[:2]:
            weave_left(rows, first, width)
        values = held("values2_%d" % N, [P, Q], F32)
        nc.gpsimd.tensor_tensor(values[:], staged[:], weights_of(3, S - Q, Q), MULT)
        put(values[:], 3, S - Q, Q)
        parts = [(flats[:, :3, lo : lo + low // 2], N + lo, low // 2) for lo in (0, low // 2)]
        for rows, first, width in parts:
            round_left(rows, 2, first, width)
        for rows, first, width in parts:
            weave_left(rows, first, width)
        for first, width in halves:
            weave_right(first, width)
        v2_w = held("v2_w", [P, S2], U32)
        nc.vector.tensor_copy(out=v2_w[:], in_=tab2_w[:].bitcast(U32).indirect(list2[:]))

        page_q = held("page_q", [P, T2], U32)
        page_s = held("page_s", [P, T2], U8)

        def quantise_page(first, width):
            cols = slice(first, first + width)
            nc.vector.quantize_mx(out=page_q[:, cols].bitcast(FP8X4), scales=page_s[:, cols], in_=woven_page(first, width).rearrange("p n t -> p (n t)"))

        cuts = [(0, N), (N, N), (2 * N, N), (3 * N, Q), (3 * N + Q, P), (T2 - P, P)]
        round_plane(gpsimd_round, 3, N, low)
        round_plane(nc.scalar.copy, 3, side, 2 * N - side)
        for first, width in cuts[2:]:
            round_plane(nc.scalar.copy, 3, first, width)
        round_plane(nc.vector.tensor_copy, 3, 0, N)
        for first, width in cuts:
            quantise_page(first, width)

        def score(b, scores, n, parts, copy):
            acc = bank(b)
            base = parts[0][0]
            for first, width in parts:
                cols = slice(first, first + width)
                mx(
                    acc[:, first - base : first - base + width], (v2_w[:, n * P : (n + 1) * P], v2_s[:, n * P : (n + 1) * P]),
                    FP8X4, page_q[:, cols], page_s[:, cols], True, True,
                )
            total = sum(width for first, width in parts)
            copy(out=scores[:, base : base + total], in_=acc[:, :total])

        for n in range(boats):
            scores = held(("scores0", "tab_w", "scores2")[n % 3], [P, T2], F32)
            if n == 0:
                for i, cut in enumerate(cuts):
                    score(i, scores, n, [cut], nc.scalar.copy if i < 3 else nc.vector.tensor_copy)
            else:
                for i, c in enumerate((3, 0, 1, 2)):
                    score((6, 3, 4, 5)[i], scores, n, [(c * N, N)], nc.scalar.copy)
            pieces = [(0, PICK)] if n < boats - 1 else [(0, N), (N, N - P), (PICK - P, P)]
            for first, width in pieces:
                picked = held(("w_raw0", "w_raw1", "wgs0")[n] if n < 3 else "picked%d" % first, [P, width], F32)
                nc.vector.tensor_tensor(picked[:], scores[:].indirect(columns(list4, first, width)), reach_sb[n][:, first : first + width], MULT)
                nc.sync.dma_start(out=out[n * P : (n + 1) * P, first : first + width], in_=picked[:])
